import numpy as np, ml_dtypes
CORES = [5,29,101,125,133,157,229,253]
N = 8
BF = ml_dtypes.bfloat16
B, S, D, SH = 1, 4096, 8192, 4
W, BC = N * B, 32
LAST = (2 * 255 * 255) >> SH
def middle(m):
    return 16 * (m % 16) + 8, 16 * (m // 16) + 8
def index(p, x, y):
    return ((x - int(p[0])) ** 2 + (y - int(p[1])) ** 2) >> SH
def loud(d, rng, cells):
    t = rng.integers(0, S, (N, 8)); sg = rng.choice(np.array([-15.0, 15.0]), 16); v = d["tr"].reshape(N, 8, 16, S); x, y = middle(np.array(cells))
    ld = sg - np.sign(sg) * rng.integers(0, 2, (N, 8, 16))
    for q in range(N):
        for g in range(8):
            d["tau"][q, g, index(d["pos"][q, g], x, y)] = t[q, g]; v[q, g, :, t[q, g]] = ld[q, g].astype(BF)
    return t, ld
def setup_inputs(rng):
    tr = rng.integers(-15, 16, (N, 128, S), dtype=np.int8).astype(np.float32).astype(BF)
    pos = rng.integers(0, 256, (N, 8, 2)).astype(np.int32)
    t = np.floor(np.sqrt(np.arange(D) / D) * (rng.random((N, 8, 1)) * 0.5 + 0.25) * S).astype(np.int64) + rng.integers(0, S // 4, (N, 8, D))
    return {"tr": tr, "pos": pos, "tau": t.astype(np.int32)}
def setup_inputs_ends(rng):
    d = setup_inputs(rng); c = np.array([[0, 0], [0, 255], [255, 0], [255, 255]])
    d["pos"] = np.stack([c[rng.permutation(8) % 4] for q in range(N)]).astype(np.int32)
    t = rng.integers(0, S, (N, 8, D)); t[:, :, 0] = 0; t[:, :, LAST] = S - 1; d["tau"] = t.astype(np.int32)
    e = rng.integers(0, 2, W); e[0] = 0; e[W - 1] = 1
    loud(d, rng, np.arange(W) * BC + e * (BC - 1)); return d
def setup_inputs_ties(rng):
    d = setup_inputs(rng); s = int(rng.integers(0, 3)); cells = []
    for k in range(W):
        z = (k + s) % 3; o = [0, BC - 1] if z == 0 else rng.choice(BC, 2, replace=False) if z == 1 else range(BC)
        cells += [k * BC + int(i) for i in o]
    loud(d, rng, cells); return d
def setup_inputs_close(rng):
    d = setup_inputs(rng); k = np.arange(W); lo = k * BC + rng.integers(0, BC // 2, W); hi = k * BC + BC // 2 + rng.integers(0, BC // 2, W); x, y = middle(lo)
    d["pos"][k % N, k // N, 0] = x; d["pos"][k % N, k // N, 1] = y
    t, ld = loud(d, rng, np.concatenate([lo, hi])); v = d["tr"].reshape(N, 8, 16, S); m = np.abs(np.sum(ld, axis=(0, 1)))
    for i in range(W):
        q, g = i % N, i // N; u = (int(t[q, g]) + int(rng.integers(1, S))) % S; h = ld[q, g].copy(); s = int(rng.integers(0, 16))
        if i % 2:
            z = [(m[a] - m[b], a, b) for a in range(16) for b in range(16) if m[a] > m[b] + 1 and abs(h[b]) < 15]
            if z:
                s, b = min(z)[1:]; h[b] = h[b] + np.sign(h[b])
        h[s] = h[s] - np.sign(h[s])
        d["tau"][q, g, 0] = u; v[q, g, :, u] = h.astype(BF)
    return d
def setup_inputs_steps(rng):
    d = setup_inputs(rng); d["pos"] = np.repeat(rng.integers(0, 256, (N, 1, 2)), 8, axis=1).astype(np.int32)
    d["tau"] = np.repeat(rng.integers(0, S, (N, 8, D // 64)), 64, axis=2).astype(np.int32); return d
def setup_inputs_spread(rng):
    d = setup_inputs(rng); a = rng.choice(np.array([0, 1, 4, 15], np.int8), (N, 8, 1, S))
    v = np.clip(rng.integers(-15, 16, (N, 8, 16, S), dtype=np.int8), -a, a)
    d["tr"] = v.reshape(N, 128, S).astype(np.float32).astype(BF)
    d["pos"] = np.floor(256 * rng.random((N, 8, 2)) ** 3).astype(np.int32); d["tau"] = np.floor(S * rng.random((N, 8, D)) ** 3).astype(np.int32); return d
def check_inputs(d):
    bad = []; v = np.asarray(d["tr"]).astype(np.float32)
    if not ((np.abs(v) <= 15) & (np.rint(v) == v)).all(): bad.append("samples")
    if not ((d["pos"] >= 0) & (d["pos"] <= 255)).all(): bad.append("places")
    if not ((d["tau"] >= 0) & (d["tau"] < S)).all(): bad.append("times")
    return bad
def focus(v, pos, tau, x, y):
    a = np.zeros((16, len(x)), np.int64)
    for q in range(N):
        for g in range(8): a += v[q, g][:, tau[q, g][index(pos[q, g], x, y)]]
    return a
def reference(tr, pos, tau):
    v = tr.astype(np.float32).astype(np.int32).reshape(N, 8, 16, S)
    x, y = middle(np.arange(256)); c = focus(v, pos, tau, x, y)
    e = np.sum(c * c, axis=0).reshape(W, BC)
    w = np.arange(W) * BC + np.argmax(e, axis=1)
    j = np.arange(256); x = (16 * (w % 16)[:, None] + j % 16).reshape(-1); y = (16 * (w // 16)[:, None] + j // 16).reshape(-1)
    fine = focus(v, pos, tau, x, y).reshape(16, N, B * 256).transpose(1, 0, 2)
    return {"y": np.ascontiguousarray(fine).astype(np.float32), "w": np.tile(w.reshape(1, 1, W), (N, 1, 1)).astype(np.float32)}

@@ -1,0 +1,393 @@
+from concourse.bass import DstId, RemoteDMATransfer
+from concourse.mybir import AluOpType as A, ActivationFunctionType as F
+
+R = 2
+SB = {
+    "float32": {"cF": [128, 40], "rowx": [128, 256], "rowb": [128, 256], "rowg": [128, 128], "rown": [128, 136], "rowm": [32, 128],
+                "rowo": [128, 32], "colp": [32, 128], "rowy": [32, 32], "zero": [32, 32], "bone": [128, 128], "dsc": [128, 256],
+                "enm": [128, 32], "uU": [32, 128], "su": [32, 128], "rr": [32, 128], "f1": [32, 32], "f2": [32, 32], "f3": [32, 32],
+                "dlt": [32, 128], "prm": [32, 8], "xy": [128, 2], "dx2": [128, 1], "dy2": [128, 16], "fx2": [128, 256],
+                "fy2": [128, 256], "pm": [128, 256], "gm": [128, 256], "sc": [128, 256], "asq": [128, 32], "rmx": [32, 32],
+                "sgn": [32, 32], "cc": [32, 1], "hb": [32, 1], "bb": [32, 1], "uq": [32, 128], "wc": [32, 1], "wrow": [1, 8],
+                "yo": [128, 32]},
+    "bfloat16": {"trS": [128, 4096], "expd": [8, 128], "zsel": [128, 136], "iden": [128, 128], "posN": [8, 2], "lU": [8, 32],
+                 "x1": [128, 256], "send1": [128, 32], "land1": [128, 256], "hop1": [128, 32], "vt": [128, 8192], "x2": [128, 2048],
+                 "sendAB": [128, 128], "sendCD": [128, 128], "hop2": [128, 128 // R], "land2": [128, 256]},
+    "int32": {"posI": [8, 2], "tauI": [128, 512], "ip": [128, 1], "cI": [128, 4], "d2l": [128, 16], "cl": [128, 16], "d2f": [128, 256],
+              "pmi": [128, 256], "d2i": [128, 128], "t1": [128, 128], "t2": [128, 128], "js": [128, 128]},
+    "uint16": {"o1": [128, 16], "o2": [128, 16], "tauU": [128, 512], "o3": [128, 128]},
+}
+SCRATCH = {n: ("sbuf", s, d) for d, b in SB.items() for n, s in b.items()}
+SCRATCH.update({"b%d" % i: ("psum", [128, 512], "float32") for i in range(8)})
+SEMAPHORES = ["cV", "cS", "cP", "cG", "dpos", "dtau", "dtr", "dw", "dy", "a1d", "a1x", "a2d", "a2x", "r1", "r2", "loc"]
+CV, GV, GS = 222, 232, (232, 236, 240, 256)
+
+
+def bits(engines):
+    return sum(1 << e for e in engines)
+
+
+def plan(T, topo, src):
+    me = T.rank_of(src)
+    cross = [q for q, c in enumerate(T.cores) if not topo.may_write(src, c)]
+    same = [q for q, c in enumerate(T.cores) if q != me and q not in cross]
+    relays = [c for c in topo.cores_of(src) if c != src and all(topo.may_write(c, T.cores[q]) for q in cross)]
+    relays = sorted(relays, key=lambda c: topo.die(c) != topo.die(src))[:R]
+    part = len(cross) // R
+    return cross, same, [(c, cross[i * part:(i + 1) * part]) for i, c in enumerate(relays)]
+
+
+def direct(T, topo, src):
+    me = T.rank_of(src)
+    cross, same, _ = plan(T, topo, src)
+    order = cross + sorted(same + [me])
+    return order, [[q for q in order[2 * P:2 * P + 2] if q != me] for P in (2, 3)]
+
+
+def dst(topo, d, src):
+    rid, pid = topo.addr(d, src)
+    return DstId(rid=rid, pnc=pid)
+
+
+def write(g, topo, core, parts, remote_sem, local_sem):
+    if len(parts) == 1:
+        d, out, src, e = parts[0]
+        rid, pid = topo.addr(d, core)
+        g.remote_dma(out, src, remote_sem, local_sem, pid, rid, bits(e))
+    else:
+        g.remote_dma_fused([RemoteDMATransfer(dst_ids=[dst(topo, d, core)], dma_engine_mask=bits(e), remote_sem=remote_sem,
+                                              srcs=[src], dsts=[out]) for d, out, src, e in parts], local_sem=local_sem)
+
+
+def relay_program(g, core, T, topo, rank, dests):
+    sem = T.sem
+    on = topo.engines(T.cores[rank], core)
+    eng = topo.engines(core, T.cores[dests[0]])
+    n = len(eng) // len(dests)
+    slot = slice(32 * rank, 32 * rank + 32)
+    to = [dst(topo, T.cores[q], core) for q in dests]
+    g.wait_ge(sem.r1, len(on) // R)
+    g.remote_dma_fused([RemoteDMATransfer(dst_ids=to, dma_engine_mask=bits(eng), remote_sem=sem.a1x, srcs=[T.hop1[:]],
+                                          dsts=[T.land1[:, slot] for _ in to])], local_sem=sem.loc)
+    g.wait_ge(sem.r2, 2 * len(on) // R)
+    write(g, topo, core, [(T.cores[q], T.land2[:, slot], T.hop2[:, 32 * i:32 * i + 32], eng[i * n:(i + 1) * n])
+                          for i, q in enumerate(dests)], sem.a2x, sem.loc)
+    g.wait_ge(sem.loc, 2 * len(eng))
+
+
+def rank_program(g, core, T, topo):
+    rank = T.rank_of(core)
+    if rank is None:
+        for q, c in enumerate(T.cores):
+            for r, dests in plan(T, topo, c)[2]:
+                if r == core:
+                    relay_program(g, core, T, topo, q, dests)
+        return
+    cross, same, relays = plan(T, topo, core)
+    order, mine = direct(T, topo, core)
+    sem = T.sem
+    eng = {"G": g, "V": g.vector, "S": g.scalar, "P": g.tensor, "Y": g.sync}
+    total = {}
+    known = {q: {} for q in eng}
+    wrote, read = {}, {}
+
+    def wait(q, name, val):
+        if known[q].get(name, 0) < val:
+            eng[q].wait_ge(sem[name], val)
+            known[q][name] = val
+
+    def order_after(q, reads, writes):
+        need = {}
+        hs = [wrote[k] for k in reads + writes if k in wrote]
+        for k in writes:
+            hs += read.get(k, [])
+        for name, val in hs:
+            need[name] = max(need.get(name, 0), val)
+        for name in sorted(need):
+            wait(q, name, need[name])
+
+    def done(ins, name, n, reads, writes):
+        total[name] = total.get(name, 0) + n
+        ins.then_inc(sem[name], n)
+        h = (name, total[name])
+        for k in reads:
+            read.setdefault(k, []).append(h)
+        for k in writes:
+            wrote[k] = h
+            read[k] = []
+
+    def op(q, call, reads, writes, *args, **kw):
+        order_after(q, reads, writes)
+        done(call(*args, **kw), "c" + q, 1, reads, writes)
+
+    def dma(q, name, out, in_, reads, writes):
+        order_after(q, reads, writes)
+        done(eng[q].dma_start(out, in_), name, 16, reads, writes)
+
+    def mm(key, out, parts, start=True, stop=True):
+        for i, (l, r, keys) in enumerate(parts):
+            a, z = start and i == 0, stop and i == len(parts) - 1
+            order_after("P", keys, [key] if a else [])
+            ins = g.tensor.matmul(out, l, r, a, z)
+        if stop:
+            done(ins, "cP", 1, [k for p in parts for k in p[2]], [key])
+
+    V, S = g.vector, g.scalar
+    ts = lambda reads, writes, *a: op("V", V.tensor_scalar, reads, writes, *a)
+    tt = lambda reads, writes, *a: op("V", V.tensor_tensor, reads, writes, *a)
+    cp = lambda reads, writes, *a: op("V", V.tensor_copy, reads, writes, *a)
+    act = lambda reads, writes, *a, **k: op("S", S.activation, reads, writes, *a, **k)
+    idn = lambda reads, writes, out, in_, scale, bias: act(reads, writes, out, in_, F.Identity, bias=bias, scale=scale)
+    iota = lambda w, out, pat, base, cm: op("G", g.iota, [], [w], out, pat, base, cm, allow_small_or_imprecise_dtypes=True)
+    fc = lambda i, n=128: T.cF[0:n, i:i + 1]
+
+    dma("Y", "dpos", T.posI[:], T.pos[:], [], ["posI"])
+    dma("S", "dtau", T.tauI[:], T.tau[:], [], ["tauI"])
+    dma("Y", "dtr", T.trS[0:64, :], T.tr[0:64, :], [], ["tr0"])
+    dma("S", "dtr", T.trS[64:128, :], T.tr[64:128, :], [], ["tr1"])
+    wrote["tr0"] = wrote["tr1"]
+
+    op("G", g.iota, [], ["ip"], T.ip[:], [[0, 1]], 0, 1)
+    iota("p", fc(0), [[0, 1]], 0, 1)
+    iota("rowg", T.rowg[:], [[1, 8], [0, 16]], 0, 0)
+    b, h4, h1 = order[0], order[4] - order[0], order[1] - order[0]
+    if all(order[i] == b + (i // 4) * h4 + (i % 4) * h1 for i in range(8)):
+        iota("rowo0", T.rowo[:], [[0, 4], [h4, 2], [h1, 4]], b, 0)
+        rowo = ["rowo0"]
+    else:
+        for i, k in enumerate(order):
+            iota("rowo%d" % i, T.rowo[:, i::8], [[0, 4]], k, 0)
+        rowo = ["rowo%d" % i for i in range(8)]
+    iota("rowx", T.rowx[:], [[0, 16], [16, 16]], 8, 0)
+    iota("rowb", T.rowb[:], [[16, 16], [0, 16]], 8, 0)
+    iota("rown", T.rown[:], [[1, 136]], 0, 0)
+    iota("rowy", T.rowy[:], [[2, 8], [0, 2], [1, 2]], 0, 0)
+    iota("rowm", T.rowm[:], [[0, 8], [1, 16]], 0, 0)
+    for P in range(4):
+        iota("colp%d" % P, T.colp[:, 32 * P:32 * P + 32], [[0, 8], [1, 2], [0, 2]], 2 * P, 0)
+    colp = ["colp%d" % P for P in range(4)]
+
+    ts(["ip"], ["i0"], T.cI[:, 0:1], T.ip[:], 15, None, A.bitwise_and)
+    ts(["ip"], ["i1"], T.cI[:, 1:2], T.ip[:], 4, None, A.logical_shift_right)
+    ts(["ip"], ["i2"], T.cI[:, 2:3], T.ip[:], 7, None, A.bitwise_and)
+    ts(["ip"], ["i3"], T.cI[:, 3:4], T.ip[:], 3, None, A.logical_shift_right)
+    cp(["i0", "i1", "i2", "i3"], ["sgkt"], T.cF[:, 1:5], T.cI[:])
+    s_, g_, k7, t_ = fc(1), fc(2), fc(3), fc(4)
+    idn(["sgkt"], ["c16"], fc(5), s_, 16.0, 8.0)
+    idn(["sgkt"], ["k16"], fc(8), k7, 1.0 / 16, 0.0)
+    idn(["sgkt"], ["s8"], fc(7), s_, 8.0, 7.0)
+    idn(["sgkt"], ["sub"], fc(6), s_, -4096.0, 15.0 * 4096)
+    act(["sgkt"], ["isA"], fc(9), t_, F.Relu, bias=1.0, scale=-1.0)
+    act(["sgkt"], ["au"], fc(11), t_, F.Abs, bias=-2.0)
+    act(["sgkt"], ["alf"], fc(10), t_, F.Relu, bias=16.0, scale=-16.0)
+    idn(["isA"], ["nA128"], fc(13), fc(9), -1.0 / 128, 1.0 / 128)
+    act(["au"], ["e2"], fc(16), fc(11), F.Relu, bias=1.0, scale=-1.0)
+    idn(["isA"], ["nA16"], fc(14), fc(9), -1.0 / 16, 1.0 / 16)
+    idn(["isA"], ["nA8"], fc(15), fc(9), 1.0 / 8, -1.0 / 8)
+    idn(["isA"], ["notA"], fc(12), fc(9), -1.0, 1.0)
+    idn(["e2", "nA128"], ["c2"], fc(20), fc(16), -3.0 / 128, fc(13))
+    ts(["rowg", "p"], ["expd"], T.expd[:], T.rowg[0:8, :], fc(0, 8), None, A.is_equal)
+    ts(["rowg", "sgkt"], ["bone"], T.bone[:], T.rowg[:], g_, None, A.is_equal)
+    op("V", V.memset, [], ["zero"], T.zero[:], 0.0)
+    ts(rowo + ["sgkt"], ["enm"], T.enm[:], T.rowo[:], k7, None, A.is_equal)
+
+    ts(["posI"], ["posN"], T.posN[:], T.posI[:], -1, None, A.mult)
+    mm("b0", T.b0[:, 0:2], [(T.expd[:], T.posN[:], ["expd", "posN"])])
+    cp(["b0"], ["xy"], T.xy[:], T.b0[:, 0:2])
+    nX, nY = T.xy[:, 0:1], T.xy[:, 1:2]
+    mm("b0", T.b0[0:32, 4:5], [(T.enm[:], fc(8), ["enm", "k16"])])
+    act(["c16", "xy"], ["dx2"], T.dx2[:], fc(5), F.Square, bias=nX)
+    act(["rowx", "xy"], ["dy2"], T.dy2[:], T.rowx[:, 0:16], F.Square, bias=nY)
+    H = lambda t, h: T[t][:, 128 * h:128 * h + 128]
+    for h in range(2):
+        act(["rowx", "xy"], ["fx2%d" % h], H("fx2", h), H("rowx", h), F.Square, bias=nX)
+        act(["rowb", "xy"], ["fy2%d" % h], H("fy2", h), H("rowb", h), F.Square, bias=nY)
+    k = lambda n, h: n + str(h)
+    ts(["rowx", "c16"], ["dsc0"], T.dsc[:], T.rowx[:], fc(5), 18.0 * 4096, A.is_gt, A.mult)
+    ts(["dy2", "dx2"], ["d2l"], T.d2l[:], T.dy2[:], T.dx2[:], None, A.add)
+    tt(["fx20", "fy20"], ["d2f0"], H("d2f", 0), H("fx2", 0), H("fy2", 0), A.add)
+    ts(["d2l"], ["cl"], T.cl[:], T.d2l[:], 4, 511, A.logical_shift_right, A.bitwise_and)
+    tt(["fx21", "fy21"], ["d2f1"], H("d2f", 1), H("fx2", 1), H("fy2", 1), A.add)
+    ts(["d2f0"], ["pmi0"], H("pmi", 0), H("d2f", 0), 13, None, A.logical_shift_right)
+    cp(["cl"], ["o1"], T.o1[:], T.cl[:])
+    ts(["d2f1"], ["pmi1"], H("pmi", 1), H("d2f", 1), 13, None, A.logical_shift_right)
+    for h in range(2):
+        ts([k("pmi", h), "sgkt"], [k("pm", h)], H("pm", h), H("pmi", h), s_, None, A.is_equal)
+    for h in range(2):
+        tt(["tauI", "o1", k("pm", h)], [k("gm", h)], H("gm", h), T.tauI[:, 0:512].indirect(T.o1[:, 8 * h:8 * h + 8]), H("pm", h), A.mult)
+        mm("b%d" % (1 + h), T["b%d" % (1 + h)][:, 0:128], [(T.bone[:], H("gm", h), ["bone", k("gm", h)])])
+    idn(["dsc0"], ["dsc"], T.dsc[:], T.dsc[:], 1.0, -17.0 * 4096)
+    idn(["sgkt", "nA16", "nA8"], ["c1"], fc(19), t_, fc(14), fc(15))
+    idn(["sgkt"], ["o8"], fc(18), t_, 8.0, -16.0)
+    idn(["e2", "isA"], ["c0"], fc(21), fc(16), 1.0, fc(9))
+    idn(["rowy", "c1", "c2"], ["f1"], T.f1[:], T.rowy[:], fc(20, 32), fc(19, 32))
+    idn(["o8", "notA"], ["o8n"], fc(22), fc(18), fc(12), 0.0)
+    idn(["posN", "rowg"], ["lUa"], T.lU[:, 0:8], T.rowg[0:8, 0:8], 0.0, T.posN[:, 0:1])
+    idn(["posN", "rowg"], ["lUb"], T.lU[:, 8:32], T.rowg[0:8, 0:24], 0.0, T.posN[:, 1:2])
+    idn(["b0"], ["k32"], fc(23, 32), T.b0[0:32, 4:5], 32.0, 0.0)
+    idn(["alf"], ["bet"], fc(17), fc(10), -17.0, 16.0)
+    idn(["k32", "notA", "o8n"], ["off"], fc(24, 32), fc(23, 32), fc(12, 32), fc(22, 32))
+    mm("b0", T.b0[0:32, 8:136], [(T.lU[:], T.expd[:], ["lUa", "lUb", "expd"])])
+
+    def scan(h):
+        op("V", V.tensor_tensor_scan, ["dsc", "b%d" % (1 + h)], ["sc%d" % h], H("sc", h), H("dsc", h),
+           T["b%d" % (1 + h)][:, 0:128], 0.0, A.add, A.max)
+
+    def pick(h):
+        ts(["sc%d" % h, "sub"], ["o2%d" % h], T.o2[:, 8 * h:8 * h + 8], T.sc[:, 128 * h + 15:128 * h + 128:16], fc(6), None, A.subtract)
+    cp(["tauI"], ["tauU"], T.tauU[:], T.tauI[:])
+    scan(0)
+    ts(["rown", "s8"], ["zsel"], T.zsel[:], T.rown[:], fc(7), None, A.is_equal)
+    pick(0)
+    scan(1)
+    tt(["f1", "rowy"], ["f2"], T.f2[:], T.f1[:], T.rowy[:], A.mult)
+    pick(1)
+    Z = lambda i: T.zsel[:, 7 - i:135 - i]
+
+    cp(["tr0", "tr1", "o20"], ["x10"], T.x1[:, 0:128], T.trS[:].indirect(T.o2[:, 0:8]))
+    act(["tr0", "tr1", "o21"], ["x11"], T.x1[:, 128:256], T.trS[:].indirect(T.o2[:, 8:16]), F.Copy)
+    mm("b3", T.b3[:, 0:32], [(Z(i), T.x1[:, 32 * i:32 * i + 32], ["zsel", "x1%d" % (i // 4)]) for i in range(8)])
+    ts(colp + ["sgkt"], ["dlt"], T.dlt[:], T.colp[:], T.cF[0:32, 3:4], None, A.is_equal)
+    ts(["f2", "c0"], ["f3"], T.f3[:], T.f2[:], fc(21, 32), None, A.add)
+    ts(["rown", "p"], ["iden"], T.iden[:], T.rown[:, 0:128], fc(0), None, A.is_equal)
+    cp(["b3"], ["send1"], T.send1[:], T.b3[:, 0:32])
+
+    on = topo.engines(core, relays[0][0])
+    off = topo.engines(core, T.cores[same[0]])
+    slot = slice(32 * rank, 32 * rank + 32)
+    order_after("G", ["send1"], [])
+    n = len(on) // R
+    write(g, topo, core, [(r, T.hop1[:], T.send1[:], on[i * n:(i + 1) * n]) for i, (r, _) in enumerate(relays)], sem.r1, sem.loc)
+    g.remote_dma_fused([RemoteDMATransfer(dst_ids=[dst(topo, T.cores[q], core) for q in same], dma_engine_mask=bits(off),
+                                          remote_sem=sem.a1d, srcs=[T.send1[:]], dsts=[T.land1[:, slot] for q in same])],
+                       local_sem=sem.loc)
+    wrote["land1d"] = ("a1d", len(same) * len(off))
+    wrote["land1x"] = ("a1x", len(cross) * len(off))
+    total["a1d"], total["a1x"] = wrote["land1d"][1], wrote["land1x"][1]
+    total["loc"] = len(on) + len(off)
+
+    table = []
+
+    def compose(q, a, b):
+        src, out, keys = T.trS[:].indirect(T.tauU[:, a:b]), T.vt[:, 16 * a:16 * b], ["tr0", "tr1", "tauU"]
+        table.append("vt%d" % a)
+        if q == "S":
+            act(keys, table[-1:], out, src, F.Copy)
+        else:
+            cp(keys, table[-1:], out, src)
+    compose("S", 256, 512)
+    ts(["rowm", "isA", "off"], ["su"], T.su[:], T.rowm[:], fc(9, 32), fc(24, 32), A.mult, A.add)
+    for P in range(4):
+        c = slice(32 * P, 32 * P + 32)
+        tt(["f3", "dlt"], ["rr%d" % P], T.rr[:, c], T.f3[:], T.dlt[:, c], A.mult)
+    tt(["b0", "su"], ["uU"], T.uU[:], T.b0[0:32, 8:136], T.su[:], A.add)
+    compose("V", 0, CV)
+
+    def sumup(key, land, own, ownkeys, name):
+        L = lambda q: land[:, 32 * q:32 * q + 32]
+        parts = [(T.iden[:], own, ["iden"] + ownkeys)] + [(T.iden[:], L(q), [name + "d"]) for q in same]
+        parts += [(T.iden[:], L(q), [name + "x"]) for q in cross]
+        mm(key, T[key][:, 0:32], parts)
+    sumup("b4", T.land1, T.send1[:], ["send1"], "land1")
+    act(["b4"], ["asq"], T.asq[:], T.b4[:, 0:32], F.Square)
+    mm("b5", T.b5[0:32, 0:32], [(T.enm[:], T.asq[:], ["enm", "asq"])])
+    compose("S", GS[0], GS[1])
+    op("V", V.tensor_tensor_scan, ["b5", "zero"], ["rmx"], T.rmx[:], T.b5[0:32, 0:32], T.zero[:], 0.0, A.max, A.max)
+    last = T.rmx[:, 31:32]
+    act(["rmx"], ["sgn", "cc"], T.sgn[:], T.rmx[:], F.Sign, bias=last, scale=-1.0, accum_out=T.cc[:])
+    compose("S", GS[1], GS[2])
+    ts(["rmx", "bet"], ["hb"], T.hb[:], T.rmx[:, 15:16], last, fc(17, 32), A.is_lt, A.mult)
+    ts(["cc", "alf", "hb"], ["bb"], T.bb[:], T.cc[:], fc(10, 32), T.hb[:], A.mult, A.add)
+    compose("V", CV, GV)
+    act(["uU", "bb"], ["uq"], T.uq[:], T.uU[:], F.Square, bias=T.bb[:])
+    compose("S", GS[2], GS[3])
+    for h in range(2):
+        mm("b%d" % (6 + h), T["b%d" % (6 + h)][:, 0:64], [(T.uq[:], T.rr[:, 64 * h:64 * h + 64], ["uq", "rr0", "rr1", "rr2", "rr3"])])
+
+    def lists(h, steps):
+        c = slice(64 * h, 64 * h + 64)
+        if 0 in steps:
+            cp(["b%d" % (6 + h)], [k("d2i", h)], T.d2i[:, c], T["b%d" % (6 + h)][:, 0:64])
+        if 1 in steps:
+            ts([k("d2i", h)], [k("t1", h)], T.t1[:, c], T.d2i[:, c], 8176, None, A.bitwise_and)
+        if 2 in steps:
+            ts([k("d2i", h)], [k("t2", h)], T.t2[:, c], T.d2i[:, c], 13, None, A.logical_shift_right)
+        if 3 in steps:
+            tt([k("t1", h), k("t2", h)], [k("js", h)], T.js[:, c], T.t1[:, c], T.t2[:, c], A.add)
+        if 4 in steps:
+            cp([k("js", h)], [k("o3", h)], T.o3[:, c], T.js[:, c])
+
+    def gather(P, q, a, b):
+        src = T.vt[:].indirect(T.o3[:, 32 * P + a:32 * P + b])
+        out = T.x2[:, 512 * P + 16 * a:512 * P + 16 * b]
+        keys, w = table + ["o3%d" % (P // 2)], ["x2%d" % (8 * P + i) for i in range(a // 4, b // 4)]
+        if q == "S":
+            act(keys, w, out, src, F.Copy)
+        else:
+            cp(keys, w, out, src)
+
+    bank = ["b1", "b2", "b3", "b0"]
+
+    def image(P, a, b):
+        mm(bank[P], T[bank[P]][:, 0:64], [(Z(i), T.x2[:, 512 * P + 64 * i:512 * P + 64 * i + 64], ["zsel", "x2%d" % (8 * P + i)])
+                                          for i in range(a, b)], a == 0, b == 8)
+
+    def stow(P, q):
+        out = (T.sendAB if P < 2 else T.sendCD)[:, 64 * (P % 2):64 * (P % 2) + 64]
+        if q == "S":
+            act([bank[P]], ["send%d" % P], out, T[bank[P]][:, 0:64], F.Copy)
+        else:
+            cp([bank[P]], ["send%d" % P], out, T[bank[P]][:, 0:64])
+
+    lists(0, (0, 1, 2, 3))
+    lists(1, (0,))
+    lists(0, (4,))
+    for a in (0, 16):
+        gather(0, "S", a, a + 16)
+        gather(1, "V", a, a + 16)
+        image(0, a // 4, a // 4 + 4)
+        image(1, a // 4, a // 4 + 4)
+    lists(1, (1, 2, 3, 4))
+    stow(0, "S")
+    stow(1, "V")
+    for P, q in ((2, "S"), (3, "V")):
+        gather(P, q, 0, 32)
+        image(P, 0, 8)
+        stow(P, q)
+
+    w = 128 // R
+    for P in range(2):
+        rs = range(P * R // 2, (P + 1) * R // 2)
+        n = len(on) // len(rs)
+        order_after("G", ["send%d" % P], [])
+        write(g, topo, core, [(relays[r][0], T.hop2[:], T.sendAB[:, w * r:w * r + w], on[i * n:(i + 1) * n])
+                              for i, r in enumerate(rs)], sem.r2, sem.loc)
+        total["loc"] += len(on)
+    for P, qs in zip((2, 3), mine):
+        n = len(off) // len(qs)
+        order_after("G", ["send%d" % P], [])
+        at = [64 * (P - 2) + 32 * (order.index(q) % 2) for q in qs]
+        write(g, topo, core, [(T.cores[q], T.land2[:, slot], T.sendCD[:, c:c + 32], off[i * n:(i + 1) * n])
+                              for i, (q, c) in enumerate(zip(qs, at))], sem.a2d, sem.loc)
+        total["loc"] += n * len(qs)
+    total["a2d"] = sum(len(off) // len(qs) for q in same for qs in direct(T, topo, T.cores[q])[1] if rank in qs)
+    total["a2x"] = len(cross) * (len(off) // (len(cross) // R))
+    wrote["land2d"], wrote["land2x"] = ("a2d", total["a2d"]), ("a2x", total["a2x"])
+
+    ts(["rown", "k32"], ["prm0"], T.prm[:], T.rown[0:32, 0:8], 32.0, fc(23, 32), A.mult, A.is_equal)
+    tt(["cc", "k32"], ["wc"], T.wc[:], T.cc[:], fc(23, 32), A.add)
+    ts(["prm0", "isA"], ["prm"], T.prm[:], T.prm[:], fc(9, 32), None, A.mult)
+    mm("b5", T.b5[0:1, 0:8], [(T.wc[:], T.prm[:], ["wc", "prm"])])
+    cp(["b5"], ["wrow"], T.wrow[:], T.b5[0:1, 0:8])
+    dma("Y", "dw", T.w[:], T.wrow[:], ["wrow"], ["w"])
+
+    i = order.index(rank)
+    c = 64 * (i // 2 - 2) + 32 * (i % 2)
+    sumup("b4", T.land2, T.sendCD[:, c:c + 32], ["send%d" % (i // 2)], "land2")
+    cp(["b4"], ["yo"], T.yo[:], T.b4[:, 0:32])
+    dma("Y", "dy", T.y[:], T.yo[:], ["yo"], ["y"])
+    wait("Y", "dw", total["dw"])
+    wait("Y", "dy", total["dy"])
+    for name in sorted(total):
+        if max(known[q].get(name, 0) for q in eng) < total[name]:
+            wait("G", name, total[name])

@@ -1,26 +1,30 @@
 from concourse.bass import DstId, RemoteDMATransfer
-from concourse.mybir import AluOpType as A, ActivationFunctionType as F
+from concourse.mybir import AluOpType as A, ActivationFunctionType as F, AxisListType as X
 
 R = 2
 SB = {
-    "float32": {"cF": [128, 40], "rowx": [128, 256], "rowb": [128, 256], "rowg": [128, 128], "rown": [128, 136], "rowm": [32, 128],
-                "rowo": [128, 32], "colp": [32, 128], "rowy": [32, 32], "zero": [32, 32], "bone": [128, 128], "dsc": [128, 256],
-                "enm": [128, 32], "uU": [32, 128], "su": [32, 128], "rr": [32, 128], "f1": [32, 32], "f2": [32, 32], "f3": [32, 32],
-                "dlt": [32, 128], "prm": [32, 8], "xy": [128, 2], "dx2": [128, 1], "dy2": [128, 16], "fx2": [128, 256],
-                "fy2": [128, 256], "pm": [128, 256], "gm": [128, 256], "sc": [128, 256], "asq": [128, 32], "rmx": [32, 32],
-                "sgn": [32, 32], "cc": [32, 1], "hb": [32, 1], "bb": [32, 1], "uq": [32, 128], "wc": [32, 1], "wrow": [1, 8],
-                "yo": [128, 32]},
-    "bfloat16": {"trS": [128, 4096], "expd": [8, 128], "zsel": [128, 136], "iden": [128, 128], "posN": [8, 2], "lU": [8, 32],
-                 "x1": [128, 256], "send1": [128, 32], "land1": [128, 256], "hop1": [128, 32], "vt": [128, 8192], "x2": [128, 2048],
-                 "sendAB": [128, 128], "sendCD": [128, 128], "hop2": [128, 128 // R], "land2": [128, 256]},
-    "int32": {"posI": [8, 2], "tauI": [128, 512], "ip": [128, 1], "cI": [128, 4], "d2l": [128, 16], "cl": [128, 16], "d2f": [128, 256],
-              "pmi": [128, 256], "d2i": [128, 128], "t1": [128, 128], "t2": [128, 128], "js": [128, 128]},
+    "float32": {"cF": [128, 8], "bone": [128, 128], "dsc": [128, 128], "enm": [128, 8], "zero": [8, 34], "xy": [128, 2],
+                "xy8": [8, 2], "dx2": [128, 2], "pm": [128, 256], "gm": [128, 256], "sc": [128, 256], "cB": [8, 33],
+                "st0": [128, 128], "stat": [128, 128], "asq": [128, 32], "rmx": [8, 34], "idf": [128, 128], "mix": [128, 128],
+                "il": [128, 256], "js": [128, 256], "cnt": [8, 3], "yo": [32, 128]},
+    "bfloat16": {"trS": [128, 4096], "rowg": [128, 128], "rowh": [8, 128], "rowm": [128, 128], "rowp": [128, 128], "rown": [128, 48],
+                 "sq": [1, 384], "ones": [128, 128], "expd": [8, 128], "lp": [8, 256], "sel": [8, 128], "zs": [128, 48],
+                 "zo": [128, 33], "iden": [128, 128], "posN": [8, 2], "posM": [8, 2], "lU": [8, 33], "cA": [1, 33], "lt": [33, 128],
+                 "wt0": [33, 128], "wt": [33, 128], "th": [8, 33], "rw": [33, 128], "low": [1, 256], "x1": [128, 256],
+                 "send1": [128, 32], "land1": [128, 256], "hop1": [128, 32], "vt": [128, 8192], "x2": [128, 2048],
+                 "send2": [128, 224], "hop2": [128, 64], "land2": [128, 256]},
+    "int32": {"posI": [8, 2], "tauI": [128, 512], "ip": [128, 1], "cI": [128, 2], "il1": [128, 16], "cl": [128, 16], "pmi": [128, 256]},
     "uint16": {"o1": [128, 16], "o2": [128, 16], "tauU": [128, 512], "o3": [128, 128]},
 }
 SCRATCH = {n: ("sbuf", s, d) for d, b in SB.items() for n, s in b.items()}
 SCRATCH.update({"b%d" % i: ("psum", [128, 512], "float32") for i in range(8)})
-SEMAPHORES = ["cV", "cS", "cP", "cG", "dpos", "dtau", "dtr", "dw", "dy", "a1d", "a1x", "a2d", "a2x", "r1", "r2", "loc"]
-CV, GV, GS = 222, 232, (232, 236, 240, 256)
+SEMAPHORES = (["cV", "cS", "cP", "cG", "dpos", "dtau", "dtr", "dw", "dy", "a1d", "a1x", "r1", "r20", "r21", "loc"]
+              + ["a2%d" % m for m in range(7)])
+STEP = (16, 8192)
+S1, VW, V1 = 220, 4, 220
+TURNS = ((0, 1), (2, 3), (4,), (5,), (6,), (7,))
+SPLIT = ((16, 32), (18, 26), (10, 16), (8, 16), (8, 16), (12, 12))
+LAST = (0, 1, 4, 5, 2, 3, 6)
 
 
 def bits(engines):
@@ -30,18 +34,22 @@ def bits(engines):
 def plan(T, topo, src):
     me = T.rank_of(src)
     cross = [q for q, c in enumerate(T.cores) if not topo.may_write(src, c)]
-    same = [q for q, c in enumerate(T.cores) if q != me and q not in cross]
+    like = [q for q in range(len(T.cores)) if q not in cross]
+    i = like.index(me)
     relays = [c for c in topo.cores_of(src) if c != src and all(topo.may_write(c, T.cores[q]) for q in cross)]
     relays = sorted(relays, key=lambda c: topo.die(c) != topo.die(src))[:R]
-    part = len(cross) // R
-    return cross, same, [(c, cross[i * part:(i + 1) * part]) for i, c in enumerate(relays)]
+    return cross[i:] + cross[:i], like[i + 1:] + like[:i], relays
 
 
-def direct(T, topo, src):
-    me = T.rank_of(src)
-    cross, same, _ = plan(T, topo, src)
-    order = cross + sorted(same + [me])
-    return order, [[q for q in order[2 * P:2 * P + 2] if q != me] for P in (2, 3)]
+def runs(order):
+    out = []
+    for m, k in enumerate(order):
+        if out and (out[-1][3] == 1 or k - order[m - 1] == out[-1][2]):
+            out[-1][2] = k - order[m - 1]
+            out[-1][3] += 1
+        else:
+            out.append([m, k, 0, 1])
+    return out
 
 
 def dst(topo, d, src):
@@ -49,47 +57,60 @@ def dst(topo, d, src):
     return DstId(rid=rid, pnc=pid)
 
 
-def write(g, topo, core, parts, remote_sem, local_sem):
+def write(g, topo, core, parts, local_sem):
+    eng = topo.engines(core, parts[0][0])
+    n = len(eng) // len(parts)
     if len(parts) == 1:
-        d, out, src, e = parts[0]
+        d, out, src, remote_sem = parts[0]
         rid, pid = topo.addr(d, core)
-        g.remote_dma(out, src, remote_sem, local_sem, pid, rid, bits(e))
+        g.remote_dma(out, src, remote_sem, local_sem, pid, rid, bits(eng))
     else:
-        g.remote_dma_fused([RemoteDMATransfer(dst_ids=[dst(topo, d, core)], dma_engine_mask=bits(e), remote_sem=remote_sem,
-                                              srcs=[src], dsts=[out]) for d, out, src, e in parts], local_sem=local_sem)
+        g.remote_dma_fused([RemoteDMATransfer(dst_ids=[dst(topo, d, core)], dma_engine_mask=bits(eng[i * n:(i + 1) * n]),
+                                              remote_sem=remote_sem, srcs=[src], dsts=[out])
+                            for i, (d, out, src, remote_sem) in enumerate(parts)], local_sem=local_sem)
+    return len(eng)
 
 
-def relay_program(g, core, T, topo, rank, dests):
+def spread(g, topo, core, cores, out, src, remote_sem, local_sem):
+    eng = topo.engines(core, cores[0])
+    g.remote_dma_fused([RemoteDMATransfer(dst_ids=[dst(topo, d, core) for d in cores], dma_engine_mask=bits(eng),
+                                          remote_sem=remote_sem, srcs=[src], dsts=[out for _ in cores])], local_sem=local_sem)
+    return len(eng)
+
+
+def share(m):
+    return [len(ms) for ms in TURNS if m in ms][0]
+
+
+def relay_program(g, core, T, topo, rank, cross, place):
     sem = T.sem
-    on = topo.engines(T.cores[rank], core)
-    eng = topo.engines(core, T.cores[dests[0]])
-    n = len(eng) // len(dests)
+    on = len(topo.engines(T.cores[rank], core))
     slot = slice(32 * rank, 32 * rank + 32)
-    to = [dst(topo, T.cores[q], core) for q in dests]
-    g.wait_ge(sem.r1, len(on) // R)
-    g.remote_dma_fused([RemoteDMATransfer(dst_ids=to, dma_engine_mask=bits(eng), remote_sem=sem.a1x, srcs=[T.hop1[:]],
-                                          dsts=[T.land1[:, slot] for _ in to])], local_sem=sem.loc)
-    g.wait_ge(sem.r2, 2 * len(on) // R)
-    write(g, topo, core, [(T.cores[q], T.land2[:, slot], T.hop2[:, 32 * i:32 * i + 32], eng[i * n:(i + 1) * n])
-                          for i, q in enumerate(dests)], sem.a2x, sem.loc)
-    g.wait_ge(sem.loc, 2 * len(eng))
+    mine = range(place, len(cross), R)
+    g.wait_ge(sem.r1, on // R)
+    n = spread(g, topo, core, [T.cores[cross[m]] for m in mine], T.land1[:, slot], T.hop1[:], sem.a1x, sem.loc)
+    for t, m in enumerate(mine):
+        g.wait_ge(sem["r2%d" % t], on // share(m))
+        n += write(g, topo, core, [(T.cores[cross[m]], T.land2[:, slot], T.hop2[:, 32 * t:32 * t + 32], sem["a2%d" % m])], sem.loc)
+    g.wait_ge(sem.loc, n)
 
 
 def rank_program(g, core, T, topo):
     rank = T.rank_of(core)
     if rank is None:
         for q, c in enumerate(T.cores):
-            for r, dests in plan(T, topo, c)[2]:
-                if r == core:
-                    relay_program(g, core, T, topo, q, dests)
+            cross, _, relays = plan(T, topo, c)
+            if core in relays:
+                relay_program(g, core, T, topo, q, cross, relays.index(core))
         return
     cross, same, relays = plan(T, topo, core)
-    order, mine = direct(T, topo, core)
+    order = cross + same + [rank]
     sem = T.sem
     eng = {"G": g, "V": g.vector, "S": g.scalar, "P": g.tensor, "Y": g.sync}
     total = {}
     known = {q: {} for q in eng}
     wrote, read = {}, {}
+    banks = ["b%d" % i for i in range(8)]
 
     def wait(q, name, val):
         if known[q].get(name, 0) < val:
@@ -117,6 +138,11 @@ def rank_program(g, core, T, topo):
             read[k] = []
 
     def op(q, call, reads, writes, *args, **kw):
+        for b in reads:
+            if b in banks:
+                for name, val in read.get(b, []):
+                    if name != "c" + q:
+                        wait(q, name, val)
         order_after(q, reads, writes)
         done(call(*args, **kw), "c" + q, 1, reads, writes)
 
@@ -124,267 +150,260 @@ def rank_program(g, core, T, topo):
         order_after(q, reads, writes)
         done(eng[q].dma_start(out, in_), name, 16, reads, writes)
 
-    def mm(key, out, parts, start=True, stop=True):
-        for i, (l, r, keys) in enumerate(parts):
-            a, z = start and i == 0, stop and i == len(parts) - 1
-            order_after("P", keys, [key] if a else [])
+    def mm(key, parts):
+        for i, (out, l, r, a, z, keys) in enumerate(parts):
+            order_after("P", keys, [key] if i == 0 and a else [])
             ins = g.tensor.matmul(out, l, r, a, z)
-        if stop:
-            done(ins, "cP", 1, [k for p in parts for k in p[2]], [key])
+        done(ins, "cP", 1, [k for p in parts for k in p[5]], [key])
+
+    def group(out, parts, start=True, stop=True):
+        return [(out, l, r, start and i == 0, stop and i == len(parts) - 1, keys) for i, (l, r, keys) in enumerate(parts)]
 
     V, S = g.vector, g.scalar
     ts = lambda reads, writes, *a: op("V", V.tensor_scalar, reads, writes, *a)
     tt = lambda reads, writes, *a: op("V", V.tensor_tensor, reads, writes, *a)
     cp = lambda reads, writes, *a: op("V", V.tensor_copy, reads, writes, *a)
+    fill = lambda w, out, c: op("V", V.memset, [], [w], out, c)
     act = lambda reads, writes, *a, **k: op("S", S.activation, reads, writes, *a, **k)
     idn = lambda reads, writes, out, in_, scale, bias: act(reads, writes, out, in_, F.Identity, bias=bias, scale=scale)
-    iota = lambda w, out, pat, base, cm: op("G", g.iota, [], [w], out, pat, base, cm, allow_small_or_imprecise_dtypes=True)
+    iota = lambda w, out, pat, base: op("G", g.iota, [], [w], out, pat, base, 0, allow_small_or_imprecise_dtypes=True)
+    keep = lambda reads, w, out, in_, pat, cmp, other, base, cm: op("G", g.affine_select, reads, [w], out, in_, pat, cmp, other, base, cm)
     fc = lambda i, n=128: T.cF[0:n, i:i + 1]
+    H = lambda t, h: T[t][:, 128 * h:128 * h + 128]
+    k = lambda n, h: n + str(h)
 
     dma("Y", "dpos", T.posI[:], T.pos[:], [], ["posI"])
     dma("S", "dtau", T.tauI[:], T.tau[:], [], ["tauI"])
-    dma("Y", "dtr", T.trS[0:64, :], T.tr[0:64, :], [], ["tr0"])
-    dma("S", "dtr", T.trS[64:128, :], T.tr[64:128, :], [], ["tr1"])
-    wrote["tr0"] = wrote["tr1"]
+    dma("Y", "dtr", T.trS[:], T.tr[:], [], ["tr"])
 
+    iota("rowm", T.rowm[:], [[0, 8], [1, 16]], 0)
     op("G", g.iota, [], ["ip"], T.ip[:], [[0, 1]], 0, 1)
-    iota("p", fc(0), [[0, 1]], 0, 1)
-    iota("rowg", T.rowg[:], [[1, 8], [0, 16]], 0, 0)
-    b, h4, h1 = order[0], order[4] - order[0], order[1] - order[0]
-    if all(order[i] == b + (i // 4) * h4 + (i % 4) * h1 for i in range(8)):
-        iota("rowo0", T.rowo[:], [[0, 4], [h4, 2], [h1, 4]], b, 0)
-        rowo = ["rowo0"]
-    else:
-        for i, k in enumerate(order):
-            iota("rowo%d" % i, T.rowo[:, i::8], [[0, 4]], k, 0)
-        rowo = ["rowo%d" % i for i in range(8)]
-    iota("rowx", T.rowx[:], [[0, 16], [16, 16]], 8, 0)
-    iota("rowb", T.rowb[:], [[16, 16], [0, 16]], 8, 0)
-    iota("rown", T.rown[:], [[1, 136]], 0, 0)
-    iota("rowy", T.rowy[:], [[2, 8], [0, 2], [1, 2]], 0, 0)
-    iota("rowm", T.rowm[:], [[0, 8], [1, 16]], 0, 0)
-    for P in range(4):
-        iota("colp%d" % P, T.colp[:, 32 * P:32 * P + 32], [[0, 8], [1, 2], [0, 2]], 2 * P, 0)
-    colp = ["colp%d" % P for P in range(4)]
-
+    iota("rowg", T.rowg[:], [[1, 8], [0, 16]], 0)
+    iota("rowh", T.rowh[:], [[1, 8], [0, 16]], 8)
+    iota("cB0", T.cB[:, 0:15], [[16, 15]], 8)
+    iota("cB2", T.cB[:, 18:33], [[16, 15]], 8)
+    iota("rown", T.rown[:], [[1, 48]], -16)
+    stretches = runs(order)
+    for m, first, step, n in stretches:
+        iota("rowp%d" % m, T.rowp[:, 16 * m:16 * (m + n)], [[32 * step, n], [1, 16]], 32 * first)
+    rowp = ["rowp%d" % r[0] for r in stretches]
+    fill("ones", T.ones[:], 1.0)
+    keep(["ones"], "iden", T.iden[:], T.ones[:], [[-1, 128]], A.is_equal, 0.0, 0, 1)
+    for i, c in enumerate((0.5 - STEP[0] // 2, -(STEP[1] // 2), 0.5, -STEP[1])):
+        fill(k("low", i), T.low[:, 64 * i:64 * i + 64], float(c))
+    fill("mix", T.mix[:], 0.0)
+    fill("cA", T.cA[:], 1.0)
+    fill("cB1", T.cB[:, 15:16], 120.0)
+    fill("mix", T.mix[:, 1::2], 1.0 / STEP[1] - 1)
+    fill("cA", T.cA[:, 16:18], 0.0)
+    cp(["ip"], ["p"], fc(0), T.ip[:])
     ts(["ip"], ["i0"], T.cI[:, 0:1], T.ip[:], 15, None, A.bitwise_and)
     ts(["ip"], ["i1"], T.cI[:, 1:2], T.ip[:], 4, None, A.logical_shift_right)
-    ts(["ip"], ["i2"], T.cI[:, 2:3], T.ip[:], 7, None, A.bitwise_and)
-    ts(["ip"], ["i3"], T.cI[:, 3:4], T.ip[:], 3, None, A.logical_shift_right)
-    cp(["i0", "i1", "i2", "i3"], ["sgkt"], T.cF[:, 1:5], T.cI[:])
-    s_, g_, k7, t_ = fc(1), fc(2), fc(3), fc(4)
-    idn(["sgkt"], ["c16"], fc(5), s_, 16.0, 8.0)
-    idn(["sgkt"], ["k16"], fc(8), k7, 1.0 / 16, 0.0)
-    idn(["sgkt"], ["s8"], fc(7), s_, 8.0, 7.0)
-    idn(["sgkt"], ["sub"], fc(6), s_, -4096.0, 15.0 * 4096)
-    act(["sgkt"], ["isA"], fc(9), t_, F.Relu, bias=1.0, scale=-1.0)
-    act(["sgkt"], ["au"], fc(11), t_, F.Abs, bias=-2.0)
-    act(["sgkt"], ["alf"], fc(10), t_, F.Relu, bias=16.0, scale=-16.0)
-    idn(["isA"], ["nA128"], fc(13), fc(9), -1.0 / 128, 1.0 / 128)
-    act(["au"], ["e2"], fc(16), fc(11), F.Relu, bias=1.0, scale=-1.0)
-    idn(["isA"], ["nA16"], fc(14), fc(9), -1.0 / 16, 1.0 / 16)
-    idn(["isA"], ["nA8"], fc(15), fc(9), 1.0 / 8, -1.0 / 8)
-    idn(["isA"], ["notA"], fc(12), fc(9), -1.0, 1.0)
-    idn(["e2", "nA128"], ["c2"], fc(20), fc(16), -3.0 / 128, fc(13))
-    ts(["rowg", "p"], ["expd"], T.expd[:], T.rowg[0:8, :], fc(0, 8), None, A.is_equal)
-    ts(["rowg", "sgkt"], ["bone"], T.bone[:], T.rowg[:], g_, None, A.is_equal)
-    op("V", V.memset, [], ["zero"], T.zero[:], 0.0)
-    ts(rowo + ["sgkt"], ["enm"], T.enm[:], T.rowo[:], k7, None, A.is_equal)
+    fill("lU3", T.lU[:, 17:18], 32.0)
+    cp(["i0", "i1"], ["sg"], T.cF[:, 1:3], T.cI[:])
+    s_, g_ = fc(1), fc(2)
+    sq = lambda i: T.sq[:, 128 * i:128 * i + 128]
+    act(["rowm"], ["sq0"], sq(0), T.rowm[0:1, :], F.Square, scale=16.0)
+    act(["rowg"], ["sq1"], sq(1), T.rowg[0:1, :], F.Square, scale=16.0)
+    act(["rowg"], ["sq2"], sq(2), T.rowg[0:1, :], F.Square, scale=16.0, bias=128.0)
+    idn(["sg"], ["sub"], fc(3), s_, -4096.0, 15.0 * 4096)
+    idn(["sg"], ["s2"], fc(5), s_, 2.0, -15.0)
 
-    ts(["posI"], ["posN"], T.posN[:], T.posI[:], -1, None, A.mult)
-    mm("b0", T.b0[:, 0:2], [(T.expd[:], T.posN[:], ["expd", "posN"])])
-    cp(["b0"], ["xy"], T.xy[:], T.b0[:, 0:2])
-    nX, nY = T.xy[:, 0:1], T.xy[:, 1:2]
-    mm("b0", T.b0[0:32, 4:5], [(T.enm[:], fc(8), ["enm", "k16"])])
-    act(["c16", "xy"], ["dx2"], T.dx2[:], fc(5), F.Square, bias=nX)
-    act(["rowx", "xy"], ["dy2"], T.dy2[:], T.rowx[:, 0:16], F.Square, bias=nY)
-    H = lambda t, h: T[t][:, 128 * h:128 * h + 128]
-    for h in range(2):
-        act(["rowx", "xy"], ["fx2%d" % h], H("fx2", h), H("rowx", h), F.Square, bias=nX)
-        act(["rowb", "xy"], ["fy2%d" % h], H("fy2", h), H("rowb", h), F.Square, bias=nY)
-    k = lambda n, h: n + str(h)
-    ts(["rowx", "c16"], ["dsc0"], T.dsc[:], T.rowx[:], fc(5), 18.0 * 4096, A.is_gt, A.mult)
-    ts(["dy2", "dx2"], ["d2l"], T.d2l[:], T.dy2[:], T.dx2[:], None, A.add)
-    tt(["fx20", "fy20"], ["d2f0"], H("d2f", 0), H("fx2", 0), H("fy2", 0), A.add)
-    ts(["d2l"], ["cl"], T.cl[:], T.d2l[:], 4, 511, A.logical_shift_right, A.bitwise_and)
-    tt(["fx21", "fy21"], ["d2f1"], H("d2f", 1), H("fx2", 1), H("fy2", 1), A.add)
-    ts(["d2f0"], ["pmi0"], H("pmi", 0), H("d2f", 0), 13, None, A.logical_shift_right)
-    cp(["cl"], ["o1"], T.o1[:], T.cl[:])
-    ts(["d2f1"], ["pmi1"], H("pmi", 1), H("d2f", 1), 13, None, A.logical_shift_right)
-    for h in range(2):
-        ts([k("pmi", h), "sgkt"], [k("pm", h)], H("pm", h), H("pmi", h), s_, None, A.is_equal)
-    for h in range(2):
-        tt(["tauI", "o1", k("pm", h)], [k("gm", h)], H("gm", h), T.tauI[:, 0:512].indirect(T.o1[:, 8 * h:8 * h + 8]), H("pm", h), A.mult)
-        mm("b%d" % (1 + h), T["b%d" % (1 + h)][:, 0:128], [(T.bone[:], H("gm", h), ["bone", k("gm", h)])])
+    ts(["rowg", "p"], ["expd"], T.expd[:], T.rowg[0:8, :], fc(0, 8), None, A.is_equal)
+    ts(["posI"], ["posN"], T.posN[:], T.posI[:], -8.0, -32.0, A.add, A.mult)
+    ts(["posI"], ["posM"], T.posM[:], T.posI[:], -8.0, -1.0 / 32, A.add, A.mult)
+    lp = lambda t: (T.lp[:, 128 * t:128 * t + 128], k("lp", t))
+    for t in range(2):
+        ts(["expd", "posN"], [lp(t)[1]], lp(t)[0], T.expd[:], T.posN[:, t:t + 1], None, A.mult)
+    one, low = T.ones[0:1, :], lambda i, n: T.low[:, 64 * i:64 * i + n]
+    qq = [(lp(t)[0], T.posM[:, t:t + 1], [lp(t)[1], "posM"]) for t in range(2)]
+    cells = lambda h: T["b%d" % (6 + h)][:, 0:128]
+    fixed = lambda h: [(one, sq(0), ["ones", "sq0"]), (one, sq(1 + h), ["ones", k("sq", 1 + h)])]
+    moved = lambda h: [(lp(0)[0], T.rowm[0:8, :], ["lp0", "rowm"]), (lp(1)[0], (T.rowg[0:8, :], T.rowh[:])[h], ["lp1", "rowg", "rowh"][:2 + h])]
+    mm("b4", group(T.b4[:, 0:1], [(sq(0), T.ones[0:1, 0:1], ["sq0", "ones"]), (one, low(0, 1), ["low0"])], stop=False))
+    mm("b3", group(T.b3[:, 0:1], [(T.rowm[0:1, :], low(3, 1), ["rowm", "low3"]), (one, low(1, 1), ["low1"]), (one, low(2, 1), ["low2"])], stop=False))
+    mm("b5", group(T.b5[:, 64:80], [(one, T.sq[:, 0:16], ["sq0"])], stop=False))
+    mm("b6", group(cells(0), fixed(0), stop=False))
+    mm("b0", [(T.b0[:, t:t + 1], lp(t)[0], T.ones[0:8, 0:1], True, True, [lp(t)[1]]) for t in range(2)])
+    mm("b4", group(T.b4[:, 0:1], qq, start=False))
+    mm("b5", group(T.b5[:, 64:80], [(lp(1)[0], T.rowm[0:8, 0:16], ["lp1"])], start=False))
+    mm("b3", group(T.b3[:, 0:1], qq, start=False))
+    mm("b6", group(cells(0), moved(0), start=False))
+    mm("b7", group(cells(1), fixed(1) + moved(1)))
+    ts(["rowg", "sg"], ["bone"], T.bone[:], T.rowg[:], g_, None, A.is_equal)
+    ts(["rowm", "sg"], ["dsc0"], T.dsc[:], T.rowm[:], s_, 18.0 * 4096, A.is_gt, A.mult)
+    idn(["posI", "posN"], ["xy8"], T.xy8[:], T.posN[:], 1.0 / 32, -8.0)
     idn(["dsc0"], ["dsc"], T.dsc[:], T.dsc[:], 1.0, -17.0 * 4096)
-    idn(["sgkt", "nA16", "nA8"], ["c1"], fc(19), t_, fc(14), fc(15))
-    idn(["sgkt"], ["o8"], fc(18), t_, 8.0, -16.0)
-    idn(["e2", "isA"], ["c0"], fc(21), fc(16), 1.0, fc(9))
-    idn(["rowy", "c1", "c2"], ["f1"], T.f1[:], T.rowy[:], fc(20, 32), fc(19, 32))
-    idn(["o8", "notA"], ["o8n"], fc(22), fc(18), fc(12), 0.0)
-    idn(["posN", "rowg"], ["lUa"], T.lU[:, 0:8], T.rowg[0:8, 0:8], 0.0, T.posN[:, 0:1])
-    idn(["posN", "rowg"], ["lUb"], T.lU[:, 8:32], T.rowg[0:8, 0:24], 0.0, T.posN[:, 1:2])
-    idn(["b0"], ["k32"], fc(23, 32), T.b0[0:32, 4:5], 32.0, 0.0)
-    idn(["alf"], ["bet"], fc(17), fc(10), -17.0, 16.0)
-    idn(["k32", "notA", "o8n"], ["off"], fc(24, 32), fc(23, 32), fc(12, 32), fc(22, 32))
-    mm("b0", T.b0[0:32, 8:136], [(T.lU[:], T.expd[:], ["lUa", "lUb", "expd"])])
+
+    row = lambda h: ts(["b%d" % (6 + h), "b3"], [k("pmi", h)], H("pmi", h), cells(h), T.b3[:, 0:1], 1.0 / STEP[1], A.add, A.mult)
+    mask = lambda h: ts([k("pmi", h)], [k("pm", h)], H("pm", h), H("pmi", h), 0.0, None, A.is_equal)
+    ts(["b0", "b4", "sg"], ["c1"], T.dx2[:, 0:1], T.b0[:, 0:1], s_, T.b4[:, 0:1], A.mult, A.add)
+    row(0)
+    ts(["b5", "c1"], ["il1"], T.il1[:], T.b5[:, 64:80], T.dx2[:, 0:1], 1.0 / STEP[0], A.add, A.mult)
+    mask(0)
+    ts(["il1"], ["cl"], T.cl[:], T.il1[:], 511, None, A.bitwise_and)
+    row(1)
+    cp(["cl"], ["o1"], T.o1[:], T.cl[:])
+    mask(1)
+    idn(["xy8", "cB0", "cB1", "cB2"], ["lU0"], T.lU[:, 0:16], T.cB[:, 0:16], 1.0, T.xy8[:, 0:1])
+    idn(["xy8", "cB2"], ["lU1"], T.lU[:, 18:33], T.cB[:, 18:33], 1.0, T.xy8[:, 0:1])
+    idn(["xy8"], ["lU2"], T.lU[:, 16:17], T.xy8[:, 1:2], 1.0, 8.0)
+    idn(["b0"], ["xy"], T.xy[:], T.b0[:, 0:2], 1.0 / 32, -8.0)
+    mm("b4", group(T.b4[0:33, 0:128], [(T.lU[:], T.expd[:], ["lU0", "lU1", "lU2", "lU3"]), (T.cA[:], T.rowm[0:1, :], ["cA"])]))
+    act(["sg", "xy"], ["dxf"], T.dx2[:, 1:2], s_, F.Square, bias=T.xy[:, 0:1])
+    for h in range(2):
+        tt(["tauI", "o1", k("pm", h)], [k("gm", h)], H("gm", h), T.tauI[:].indirect(T.o1[:, 8 * h:8 * h + 8]), H("pm", h), A.mult)
+        mm("b%d" % (1 + h), group(T["b%d" % (1 + h)][:, 0:128], [(T.bone[:], H("gm", h), ["bone", k("gm", h)])]))
+    narrow = lambda h: cp(["tauI"], [k("tauU", h)], T.tauU[:, 256 * h:256 * h + 256], T.tauI[:, 256 * h:256 * h + 256])
+    narrow(0)
+
+    act(rowp + ["xy"], ["st0"], T.st0[:], T.rowp[:], F.Square, bias=T.xy[:, 1:2])
+    act(["b4"], ["lt"], T.lt[:], T.b4[0:33, 0:128], F.Copy)
+    idn(["st0", "dxf"], ["stat"], T.stat[:], T.st0[:], 1.0, T.dx2[:, 1:2])
+    act(["iden"], ["idf"], T.idf[:], T.iden[:], F.Copy)
 
     def scan(h):
-        op("V", V.tensor_tensor_scan, ["dsc", "b%d" % (1 + h)], ["sc%d" % h], H("sc", h), H("dsc", h),
+        op("V", V.tensor_tensor_scan, ["dsc", "b%d" % (1 + h)], ["sc%d" % h], H("sc", h), T.dsc[:],
            T["b%d" % (1 + h)][:, 0:128], 0.0, A.add, A.max)
 
     def pick(h):
-        ts(["sc%d" % h, "sub"], ["o2%d" % h], T.o2[:, 8 * h:8 * h + 8], T.sc[:, 128 * h + 15:128 * h + 128:16], fc(6), None, A.subtract)
-    cp(["tauI"], ["tauU"], T.tauU[:], T.tauI[:])
+        ts(["sc%d" % h, "sub"], ["o2%d" % h], T.o2[:, 8 * h:8 * h + 8], T.sc[:, 128 * h + 15:128 * h + 128:16], fc(3), None, A.subtract)
     scan(0)
-    ts(["rown", "s8"], ["zsel"], T.zsel[:], T.rown[:], fc(7), None, A.is_equal)
+    ts(["rown", "sg"], ["zs"], T.zs[:], T.rown[:], s_, None, A.is_equal)
     pick(0)
     scan(1)
-    tt(["f1", "rowy"], ["f2"], T.f2[:], T.f1[:], T.rowy[:], A.mult)
+    ts(["rowm", "sg"], ["enm"], T.enm[:], T.rowm[:, 0:8], g_, None, A.is_equal)
     pick(1)
-    Z = lambda i: T.zsel[:, 7 - i:135 - i]
+    ts(["rown", "s2"], ["zo"], T.zo[:], T.rown[:, 0:33], fc(5), None, A.is_equal)
 
-    cp(["tr0", "tr1", "o20"], ["x10"], T.x1[:, 0:128], T.trS[:].indirect(T.o2[:, 0:8]))
-    act(["tr0", "tr1", "o21"], ["x11"], T.x1[:, 128:256], T.trS[:].indirect(T.o2[:, 8:16]), F.Copy)
-    mm("b3", T.b3[:, 0:32], [(Z(i), T.x1[:, 32 * i:32 * i + 32], ["zsel", "x1%d" % (i // 4)]) for i in range(8)])
-    ts(colp + ["sgkt"], ["dlt"], T.dlt[:], T.colp[:], T.cF[0:32, 3:4], None, A.is_equal)
-    ts(["f2", "c0"], ["f3"], T.f3[:], T.f2[:], fc(21, 32), None, A.add)
-    ts(["rown", "p"], ["iden"], T.iden[:], T.rown[:, 0:128], fc(0), None, A.is_equal)
-    cp(["b3"], ["send1"], T.send1[:], T.b3[:, 0:32])
-
-    on = topo.engines(core, relays[0][0])
-    off = topo.engines(core, T.cores[same[0]])
-    slot = slice(32 * rank, 32 * rank + 32)
-    order_after("G", ["send1"], [])
-    n = len(on) // R
-    write(g, topo, core, [(r, T.hop1[:], T.send1[:], on[i * n:(i + 1) * n]) for i, (r, _) in enumerate(relays)], sem.r1, sem.loc)
-    g.remote_dma_fused([RemoteDMATransfer(dst_ids=[dst(topo, T.cores[q], core) for q in same], dma_engine_mask=bits(off),
-                                          remote_sem=sem.a1d, srcs=[T.send1[:]], dsts=[T.land1[:, slot] for q in same])],
-                       local_sem=sem.loc)
-    wrote["land1d"] = ("a1d", len(same) * len(off))
-    wrote["land1x"] = ("a1x", len(cross) * len(off))
-    total["a1d"], total["a1x"] = wrote["land1d"][1], wrote["land1x"][1]
-    total["loc"] = len(on) + len(off)
+    act(["tr", "o20"], ["x10"], T.x1[:, 0:128], T.trS[:].indirect(T.o2[:, 0:8]), F.Copy)
+    cp(["tr", "o21"], ["x11"], T.x1[:, 128:256], T.trS[:].indirect(T.o2[:, 8:16]))
+    mm("b3", [p for Q in range(4) for p in group(T.b3[32 * Q:32 * Q + 32, 0:32], [
+        (T.zs[:, 16 - 16 * j:48 - 16 * j], T.x1[:, 64 * Q + 32 * j:64 * Q + 32 * j + 32], ["zs", "x1%d" % (Q // 2)]) for j in range(2)])])
 
     table = []
 
     def compose(q, a, b):
-        src, out, keys = T.trS[:].indirect(T.tauU[:, a:b]), T.vt[:, 16 * a:16 * b], ["tr0", "tr1", "tauU"]
+        src, out = T.trS[:].indirect(T.tauU[:, a:b]), T.vt[:, 16 * a:16 * b]
+        keys = ["tr"] + [k("tauU", h) for h in range(a // 256, (b - 1) // 256 + 1)]
         table.append("vt%d" % a)
         if q == "S":
             act(keys, table[-1:], out, src, F.Copy)
         else:
             cp(keys, table[-1:], out, src)
-    compose("S", 256, 512)
-    ts(["rowm", "isA", "off"], ["su"], T.su[:], T.rowm[:], fc(9, 32), fc(24, 32), A.mult, A.add)
-    for P in range(4):
-        c = slice(32 * P, 32 * P + 32)
-        tt(["f3", "dlt"], ["rr%d" % P], T.rr[:, c], T.f3[:], T.dlt[:, c], A.mult)
-    tt(["b0", "su"], ["uU"], T.uU[:], T.b0[0:32, 8:136], T.su[:], A.add)
-    compose("V", 0, CV)
+    cuts = [0, S1, S1 + V1, S1 + V1 + VW, S1 + V1 + 2 * VW, 512]
+    compose("S", cuts[0], cuts[1])
+    narrow(1)
+    cp(["b3"], ["send1"], T.send1[:], T.b3[:, 0:32])
+    fill("b5", T.b5[0:8, 16:18], 0.0)
+    fill("zero", T.zero[:], 0.0)
+    compose("V", cuts[1], cuts[2])
 
-    def sumup(key, land, own, ownkeys, name):
-        L = lambda q: land[:, 32 * q:32 * q + 32]
-        parts = [(T.iden[:], own, ["iden"] + ownkeys)] + [(T.iden[:], L(q), [name + "d"]) for q in same]
-        parts += [(T.iden[:], L(q), [name + "x"]) for q in cross]
-        mm(key, T[key][:, 0:32], parts)
-    sumup("b4", T.land1, T.send1[:], ["send1"], "land1")
-    act(["b4"], ["asq"], T.asq[:], T.b4[:, 0:32], F.Square)
-    mm("b5", T.b5[0:32, 0:32], [(T.enm[:], T.asq[:], ["enm", "asq"])])
-    compose("S", GS[0], GS[1])
-    op("V", V.tensor_tensor_scan, ["b5", "zero"], ["rmx"], T.rmx[:], T.b5[0:32, 0:32], T.zero[:], 0.0, A.max, A.max)
-    last = T.rmx[:, 31:32]
-    act(["rmx"], ["sgn", "cc"], T.sgn[:], T.rmx[:], F.Sign, bias=last, scale=-1.0, accum_out=T.cc[:])
-    compose("S", GS[1], GS[2])
-    ts(["rmx", "bet"], ["hb"], T.hb[:], T.rmx[:, 15:16], last, fc(17, 32), A.is_lt, A.mult)
-    ts(["cc", "alf", "hb"], ["bb"], T.bb[:], T.cc[:], fc(10, 32), T.hb[:], A.mult, A.add)
-    compose("V", CV, GV)
-    act(["uU", "bb"], ["uq"], T.uq[:], T.uU[:], F.Square, bias=T.bb[:])
-    compose("S", GS[2], GS[3])
+    slot = slice(32 * rank, 32 * rank + 32)
+    off = len(topo.engines(core, T.cores[same[0]]))
+    order_after("G", ["send1"], [])
+    total["loc"] = write(g, topo, core, [(r, T.hop1[:], T.send1[:], sem.r1) for r in relays], sem.loc)
+    total["loc"] += spread(g, topo, core, [T.cores[q] for q in same], T.land1[:, slot], T.send1[:], sem.a1d, sem.loc)
+    total.update({"a1d": len(same) * off, "a1x": len(cross) * off})
+    total.update({"a2%d" % m: off // (1 if m < len(cross) else share(m)) for m in range(7)})
+    wrote.update({name: (name, n) for name, n in total.items() if name[0] == "a"})
+    for m, first, step, n in stretches:
+        c = slice(16 * m, 16 * (m + n))
+        keep(["ones"], "sel%d" % m, T.sel[:, c], T.ones[0:8, c], [[step, n], [0, 16]], A.is_equal, 0.0, first, -1)
+    sel = ["sel%d" % r[0] for r in stretches]
+    keep(rowp, "wt0", T.wt0[:], T.rowp[0:33, :], [[0, 128]], A.is_equal, 32.0, -17, 1)
+    keep(["wt0"], "wt", T.wt[:], T.wt0[:], [[0, 128]], A.not_equal, -480.0, -15, 1)
+
+    dist = [["b0", "b1"], ["b2", "b3"]]
     for h in range(2):
-        mm("b%d" % (6 + h), T["b%d" % (6 + h)][:, 0:64], [(T.uq[:], T.rr[:, 64 * h:64 * h + 64], ["uq", "rr0", "rr1", "rr2", "rr3"])])
-
-    def lists(h, steps):
+        for i, b in enumerate(dist[h]):
+            mm(b, group(T[b][:, 0:64], [(T.idf[:], T.stat[:, 64 * h:64 * h + 64], ["idf", "stat"])] + [
+                (one, low(j, 64), []) for j in ((0,), (1, 2))[i]], stop=False))
+    L = lambda land, q: land[:, 32 * q:32 * q + 32]
+    mm("b4", group(T.b4[:, 0:32], [(T.iden[:], T.send1[:], ["iden", "send1"])] + [(T.iden[:], L(T.land1, q), ["a1d"]) for q in same]
+                   + [(T.iden[:], L(T.land1, q), ["a1x"]) for q in cross]))
+    act(["b4"], ["asq"], T.asq[:], T.b4[:, 0:32], F.Square)
+    compose("S", cuts[4], cuts[5])
+    mm("b5", [(T.b5[0:8, 18 * h:18 * h + 16], T.enm[:], T.asq[:, 16 * h:16 * h + 16], True, True, ["enm", "asq"]) for h in range(2)])
+    op("V", V.tensor_tensor_scan, ["b5", "zero"], ["rmx"], T.rmx[:], T.b5[0:8, 0:34], T.zero[:], 0.0, A.max, A.max)
+    ts(["rmx"], ["th"], T.th[:], T.rmx[:, 0:33], T.rmx[:, 33:34], None, A.is_lt)
+    turned = ["b6", "b4"]
+    for h in range(2):
+        mm(turned[h], group(T[turned[h]][0:33, 0:64], [(T.th[:], T.sel[:, 64 * h:64 * h + 64], ["th"] + sel)]))
+    compose("V", cuts[2], cuts[3])
+    for h in range(2):
         c = slice(64 * h, 64 * h + 64)
-        if 0 in steps:
-            cp(["b%d" % (6 + h)], [k("d2i", h)], T.d2i[:, c], T["b%d" % (6 + h)][:, 0:64])
-        if 1 in steps:
-            ts([k("d2i", h)], [k("t1", h)], T.t1[:, c], T.d2i[:, c], 8176, None, A.bitwise_and)
-        if 2 in steps:
-            ts([k("d2i", h)], [k("t2", h)], T.t2[:, c], T.d2i[:, c], 13, None, A.logical_shift_right)
-        if 3 in steps:
-            tt([k("t1", h), k("t2", h)], [k("js", h)], T.js[:, c], T.t1[:, c], T.t2[:, c], A.add)
-        if 4 in steps:
-            cp([k("js", h)], [k("o3", h)], T.o3[:, c], T.js[:, c])
+        tt([turned[h], "wt"], [k("rw", h)], T.rw[:, c], T[turned[h]][0:33, 0:64], T.wt[:, c], A.mult)
+        for b in dist[h]:
+            mm(b, group(T[b][:, 0:64], [(T.lt[:], T.rw[:, c], ["lt", k("rw", h)])], start=False))
+    compose("V", cuts[3], cuts[4])
 
-    def gather(P, q, a, b):
-        src = T.vt[:].indirect(T.o3[:, 32 * P + a:32 * P + b])
-        out = T.x2[:, 512 * P + 16 * a:512 * P + 16 * b]
-        keys, w = table + ["o3%d" % (P // 2)], ["x2%d" % (8 * P + i) for i in range(a // 4, b // 4)]
+    def lists(h, step):
+        a, c = 128 * h, slice(128 * h, 128 * h + 128)
+        if step < 2:
+            b, big = dist[h][step], 1.5 * 2.0 ** 23 * STEP[step]
+            ts([b], ["il%d%d" % (h, step)], T.il[:, a + 1 - step:a + 128:2], T[b][:, 0:64], big, big, A.add, A.subtract)
+        elif step == 2:
+            op("V", V.tensor_tensor_scan, ["mix", "il%d0" % h, "il%d1" % h], [k("js", h)], T.js[:, c], T.mix[:], T.il[:, c], 0.0, A.mult, A.add)
+        else:
+            cp([k("js", h)], [k("o3", h)], T.o3[:, 64 * h:64 * h + 64], T.js[:, a + 1:a + 128:2])
+
+    made = {}
+
+    def gather(q, a, b):
+        if a == b:
+            return
+        src, out = T.vt[:].indirect(T.o3[:, a:b]), T.x2[:, 16 * a:16 * b]
+        keys, w = table + ["o3%d" % (a // 64)], ["x2%d" % a]
+        for h in range(a // 8, (b + 7) // 8):
+            made.setdefault(h, []).append(w[0])
         if q == "S":
             act(keys, w, out, src, F.Copy)
         else:
             cp(keys, w, out, src)
 
-    bank = ["b1", "b2", "b3", "b0"]
+    bank = ["b7", "b5", "b6", "b0"]
+    samples = lambda m, h: T.x2[:, 128 * (2 * m + h):128 * (2 * m + h + 1)]
 
-    def image(P, a, b):
-        mm(bank[P], T[bank[P]][:, 0:64], [(Z(i), T.x2[:, 512 * P + 64 * i:512 * P + 64 * i + 64], ["zsel", "x2%d" % (8 * P + i)])
-                                          for i in range(a, b)], a == 0, b == 8)
+    def images(t):
+        b = bank[t % 4]
+        mm(b, [(T[b][:, 32 * i + h:32 * i + 32:2], samples(m, h), T.zs[:, 16:32], True, True, ["zs"] + made[2 * m + h])
+               for i, m in enumerate(TURNS[t]) for h in range(2)])
 
-    def stow(P, q):
-        out = (T.sendAB if P < 2 else T.sendCD)[:, 64 * (P % 2):64 * (P % 2) + 64]
-        if q == "S":
-            act([bank[P]], ["send%d" % P], out, T[bank[P]][:, 0:64], F.Copy)
-        else:
-            cp([bank[P]], ["send%d" % P], out, T[bank[P]][:, 0:64])
+    def send(t):
+        ms, b = TURNS[t], bank[t % 4]
+        cp([b], ["send%d" % t], T.send2[:, 32 * ms[0]:32 * ms[-1] + 32], T[b][:, 0:32 * len(ms)])
+        order_after("G", ["send%d" % t], [])
+        to = lambda m: ((relays[m % R], L(T.hop2, m // R), L(T.send2, m), sem["r2%d" % (m // R)]) if m < len(cross)
+                        else (T.cores[order[m]], T.land2[:, slot], L(T.send2, m), sem["a2%d" % m]))
+        total["loc"] += write(g, topo, core, [to(m) for m in ms], sem.loc)
 
-    lists(0, (0, 1, 2, 3))
-    lists(1, (0,))
-    lists(0, (4,))
-    for a in (0, 16):
-        gather(0, "S", a, a + 16)
-        gather(1, "V", a, a + 16)
-        image(0, a // 4, a // 4 + 4)
-        image(1, a // 4, a // 4 + 4)
-    lists(1, (1, 2, 3, 4))
-    stow(0, "S")
-    stow(1, "V")
-    for P, q in ((2, "S"), (3, "V")):
-        gather(P, q, 0, 32)
-        image(P, 0, 8)
-        stow(P, q)
+    for h, step in ((0, 0), (0, 1), (1, 0), (0, 2), (1, 1), (0, 3)):
+        lists(h, step)
+    for t, (ms, (a, b)) in enumerate(zip(TURNS, SPLIT)):
+        lo, hi = 16 * ms[0], 16 * ms[-1] + 16
+        gather("S", lo, lo + a)
+        gather("V", lo + a, lo + b)
+        if t > 0:
+            send(t - 1)
+        if t == 1:
+            lists(1, 3)
+        gather("V", lo + b, hi)
+        if t == 0:
+            lists(1, 2)
+        if rank != order[ms[0]]:
+            images(t)
 
-    w = 128 // R
-    for P in range(2):
-        rs = range(P * R // 2, (P + 1) * R // 2)
-        n = len(on) // len(rs)
-        order_after("G", ["send%d" % P], [])
-        write(g, topo, core, [(relays[r][0], T.hop2[:], T.sendAB[:, w * r:w * r + w], on[i * n:(i + 1) * n])
-                              for i, r in enumerate(rs)], sem.r2, sem.loc)
-        total["loc"] += len(on)
-    for P, qs in zip((2, 3), mine):
-        n = len(off) // len(qs)
-        order_after("G", ["send%d" % P], [])
-        at = [64 * (P - 2) + 32 * (order.index(q) % 2) for q in qs]
-        write(g, topo, core, [(T.cores[q], T.land2[:, slot], T.sendCD[:, c:c + 32], off[i * n:(i + 1) * n])
-                              for i, (q, c) in enumerate(zip(qs, at))], sem.a2d, sem.loc)
-        total["loc"] += n * len(qs)
-    total["a2d"] = sum(len(off) // len(qs) for q in same for qs in direct(T, topo, T.cores[q])[1] if rank in qs)
-    total["a2x"] = len(cross) * (len(off) // (len(cross) // R))
-    wrote["land2d"], wrote["land2x"] = ("a2d", total["a2d"]), ("a2x", total["a2x"])
+    op("V", V.tensor_reduce, ["th"], ["cnt0"], T.cnt[:, 0:1], T.th[:], X.X, A.add)
+    ts(["th", "cnt0"], ["cnt1"], T.cnt[:, 1:2], T.th[:, 15:16], -2.0, T.cnt[:, 0:1], A.mult, A.add)
+    ts(["p", "cnt1"], ["cnt2"], T.cnt[:, 2:3], fc(0, 8), 32.0, T.cnt[:, 1:2], A.mult, A.add)
+    dma("Y", "dw", T.w[:], T.cnt[:, 2:3], ["cnt2"], ["w"])
 
-    ts(["rown", "k32"], ["prm0"], T.prm[:], T.rown[0:32, 0:8], 32.0, fc(23, 32), A.mult, A.is_equal)
-    tt(["cc", "k32"], ["wc"], T.wc[:], T.cc[:], fc(23, 32), A.add)
-    ts(["prm0", "isA"], ["prm"], T.prm[:], T.prm[:], fc(9, 32), None, A.mult)
-    mm("b5", T.b5[0:1, 0:8], [(T.wc[:], T.prm[:], ["wc", "prm"])])
-    cp(["b5"], ["wrow"], T.wrow[:], T.b5[0:1, 0:8])
-    dma("Y", "dw", T.w[:], T.wrow[:], ["wrow"], ["w"])
-
-    i = order.index(rank)
-    c = 64 * (i // 2 - 2) + 32 * (i % 2)
-    sumup("b4", T.land2, T.sendCD[:, c:c + 32], ["send%d" % (i // 2)], "land2")
-    cp(["b4"], ["yo"], T.yo[:], T.b4[:, 0:32])
+    parts = [(T.zo[:, 1 - h:33 - h], samples(7, h), ["zo"] + made[14 + h]) for h in range(2)]
+    sender = {sum(plan(T, topo, c)[:2], []).index(rank): q for q, c in enumerate(T.cores) if q != rank}
+    parts += [(L(T.land2, sender[m]), T.iden[:], ["iden", "a2%d" % m]) for m in LAST]
+    mm("b4", group(T.b4[0:32, 0:128], parts))
+    cp(["b4"], ["yo"], T.yo[:], T.b4[0:32, 0:128])
     dma("Y", "dy", T.y[:], T.yo[:], ["yo"], ["y"])
     wait("Y", "dw", total["dw"])
     wait("Y", "dy", total["dy"])

from concourse.bass import DstId, RemoteDMATransfer
from concourse.mybir import AluOpType as A, ActivationFunctionType as F, AxisListType as X

R = 2
SB = {
    "float32": {"cF": [128, 8], "bone": [128, 128], "dsc": [128, 128], "enm": [128, 8], "zero": [8, 34], "xy": [128, 2],
                "xy8": [8, 2], "dx2": [128, 2], "pm": [128, 256], "gm": [128, 256], "sc": [128, 256], "cB": [8, 33],
                "st0": [128, 128], "stat": [128, 128], "asq": [128, 32], "rmx": [8, 34], "idf": [128, 128], "mix": [128, 128],
                "il": [128, 256], "js": [128, 256], "cnt": [8, 3], "yo": [32, 128]},
    "bfloat16": {"trS": [128, 4096], "rowg": [128, 128], "rowh": [8, 128], "rowm": [128, 128], "rowp": [128, 128], "rown": [128, 48],
                 "sq": [1, 384], "ones": [128, 128], "expd": [8, 128], "lp": [8, 256], "sel": [8, 128], "zs": [128, 48],
                 "zo": [128, 33], "iden": [128, 128], "posN": [8, 2], "posM": [8, 2], "lU": [8, 33], "cA": [1, 33], "lt": [33, 128],
                 "wt0": [33, 128], "wt": [33, 128], "th": [8, 33], "rw": [33, 128], "low": [1, 256], "x1": [128, 256],
                 "send1": [128, 32], "land1": [128, 256], "hop1": [128, 32], "vt": [128, 8192], "x2": [128, 2048],
                 "send2": [128, 224], "hop2": [128, 64], "land2": [128, 256]},
    "int32": {"posI": [8, 2], "tauI": [128, 512], "ip": [128, 1], "cI": [128, 2], "il1": [128, 16], "cl": [128, 16], "pmi": [128, 256]},
    "uint16": {"o1": [128, 16], "o2": [128, 16], "tauU": [128, 512], "o3": [128, 128]},
}
SCRATCH = {n: ("sbuf", s, d) for d, b in SB.items() for n, s in b.items()}
SCRATCH.update({"b%d" % i: ("psum", [128, 512], "float32") for i in range(8)})
SEMAPHORES = (["cV", "cS", "cP", "cG", "dpos", "dtau", "dtr", "dw", "dy", "a1d", "a1x", "r1", "r20", "r21", "loc"]
              + ["a2%d" % m for m in range(7)])
STEP = (16, 8192)
S1, VW, V1 = 220, 4, 220
TURNS = ((0, 1), (2, 3), (4,), (5,), (6,), (7,))
SPLIT = ((16, 32), (18, 26), (10, 16), (8, 16), (8, 16), (12, 12))
LAST = (0, 1, 4, 5, 2, 3, 6)


def bits(engines):
    return sum(1 << e for e in engines)


def plan(T, topo, src):
    me = T.rank_of(src)
    cross = [q for q, c in enumerate(T.cores) if not topo.may_write(src, c)]
    like = [q for q in range(len(T.cores)) if q not in cross]
    i = like.index(me)
    relays = [c for c in topo.cores_of(src) if c != src and all(topo.may_write(c, T.cores[q]) for q in cross)]
    relays = sorted(relays, key=lambda c: topo.die(c) != topo.die(src))[:R]
    return cross[i:] + cross[:i], like[i + 1:] + like[:i], relays


def runs(order):
    out = []
    for m, k in enumerate(order):
        if out and (out[-1][3] == 1 or k - order[m - 1] == out[-1][2]):
            out[-1][2] = k - order[m - 1]
            out[-1][3] += 1
        else:
            out.append([m, k, 0, 1])
    return out


def dst(topo, d, src):
    rid, pid = topo.addr(d, src)
    return DstId(rid=rid, pnc=pid)


def write(g, topo, core, parts, local_sem):
    eng = topo.engines(core, parts[0][0])
    n = len(eng) // len(parts)
    if len(parts) == 1:
        d, out, src, remote_sem = parts[0]
        rid, pid = topo.addr(d, core)
        g.remote_dma(out, src, remote_sem, local_sem, pid, rid, bits(eng))
    else:
        g.remote_dma_fused([RemoteDMATransfer(dst_ids=[dst(topo, d, core)], dma_engine_mask=bits(eng[i * n:(i + 1) * n]),
                                              remote_sem=remote_sem, srcs=[src], dsts=[out])
                            for i, (d, out, src, remote_sem) in enumerate(parts)], local_sem=local_sem)
    return len(eng)


def spread(g, topo, core, cores, out, src, remote_sem, local_sem):
    eng = topo.engines(core, cores[0])
    g.remote_dma_fused([RemoteDMATransfer(dst_ids=[dst(topo, d, core) for d in cores], dma_engine_mask=bits(eng),
                                          remote_sem=remote_sem, srcs=[src], dsts=[out for _ in cores])], local_sem=local_sem)
    return len(eng)


def share(m):
    return [len(ms) for ms in TURNS if m in ms][0]


def relay_program(g, core, T, topo, rank, cross, place):
    sem = T.sem
    on = len(topo.engines(T.cores[rank], core))
    slot = slice(32 * rank, 32 * rank + 32)
    mine = range(place, len(cross), R)
    g.wait_ge(sem.r1, on // R)
    n = spread(g, topo, core, [T.cores[cross[m]] for m in mine], T.land1[:, slot], T.hop1[:], sem.a1x, sem.loc)
    for t, m in enumerate(mine):
        g.wait_ge(sem["r2%d" % t], on // share(m))
        n += write(g, topo, core, [(T.cores[cross[m]], T.land2[:, slot], T.hop2[:, 32 * t:32 * t + 32], sem["a2%d" % m])], sem.loc)
    g.wait_ge(sem.loc, n)


def rank_program(g, core, T, topo):
    rank = T.rank_of(core)
    if rank is None:
        for q, c in enumerate(T.cores):
            cross, _, relays = plan(T, topo, c)
            if core in relays:
                relay_program(g, core, T, topo, q, cross, relays.index(core))
        return
    cross, same, relays = plan(T, topo, core)
    order = cross + same + [rank]
    sem = T.sem
    eng = {"G": g, "V": g.vector, "S": g.scalar, "P": g.tensor, "Y": g.sync}
    total = {}
    known = {q: {} for q in eng}
    wrote, read = {}, {}
    banks = ["b%d" % i for i in range(8)]

    def wait(q, name, val):
        if known[q].get(name, 0) < val:
            eng[q].wait_ge(sem[name], val)
            known[q][name] = val

    def order_after(q, reads, writes):
        need = {}
        hs = [wrote[k] for k in reads + writes if k in wrote]
        for k in writes:
            hs += read.get(k, [])
        for name, val in hs:
            need[name] = max(need.get(name, 0), val)
        for name in sorted(need):
            wait(q, name, need[name])

    def done(ins, name, n, reads, writes):
        total[name] = total.get(name, 0) + n
        ins.then_inc(sem[name], n)
        h = (name, total[name])
        for k in reads:
            read.setdefault(k, []).append(h)
        for k in writes:
            wrote[k] = h
            read[k] = []

    def op(q, call, reads, writes, *args, **kw):
        for b in reads:
            if b in banks:
                for name, val in read.get(b, []):
                    if name != "c" + q:
                        wait(q, name, val)
        order_after(q, reads, writes)
        done(call(*args, **kw), "c" + q, 1, reads, writes)

    def dma(q, name, out, in_, reads, writes):
        order_after(q, reads, writes)
        done(eng[q].dma_start(out, in_), name, 16, reads, writes)

    def mm(key, parts):
        for i, (out, l, r, a, z, keys) in enumerate(parts):
            order_after("P", keys, [key] if i == 0 and a else [])
            ins = g.tensor.matmul(out, l, r, a, z)
        done(ins, "cP", 1, [k for p in parts for k in p[5]], [key])

    def group(out, parts, start=True, stop=True):
        return [(out, l, r, start and i == 0, stop and i == len(parts) - 1, keys) for i, (l, r, keys) in enumerate(parts)]

    V, S = g.vector, g.scalar
    ts = lambda reads, writes, *a: op("V", V.tensor_scalar, reads, writes, *a)
    tt = lambda reads, writes, *a: op("V", V.tensor_tensor, reads, writes, *a)
    cp = lambda reads, writes, *a: op("V", V.tensor_copy, reads, writes, *a)
    fill = lambda w, out, c: op("V", V.memset, [], [w], out, c)
    act = lambda reads, writes, *a, **k: op("S", S.activation, reads, writes, *a, **k)
    idn = lambda reads, writes, out, in_, scale, bias: act(reads, writes, out, in_, F.Identity, bias=bias, scale=scale)
    iota = lambda w, out, pat, base: op("G", g.iota, [], [w], out, pat, base, 0, allow_small_or_imprecise_dtypes=True)
    keep = lambda reads, w, out, in_, pat, cmp, other, base, cm: op("G", g.affine_select, reads, [w], out, in_, pat, cmp, other, base, cm)
    fc = lambda i, n=128: T.cF[0:n, i:i + 1]
    H = lambda t, h: T[t][:, 128 * h:128 * h + 128]
    k = lambda n, h: n + str(h)

    dma("Y", "dpos", T.posI[:], T.pos[:], [], ["posI"])
    dma("S", "dtau", T.tauI[:], T.tau[:], [], ["tauI"])
    dma("Y", "dtr", T.trS[:], T.tr[:], [], ["tr"])

    iota("rowm", T.rowm[:], [[0, 8], [1, 16]], 0)
    op("G", g.iota, [], ["ip"], T.ip[:], [[0, 1]], 0, 1)
    iota("rowg", T.rowg[:], [[1, 8], [0, 16]], 0)
    iota("rowh", T.rowh[:], [[1, 8], [0, 16]], 8)
    iota("cB0", T.cB[:, 0:15], [[16, 15]], 8)
    iota("cB2", T.cB[:, 18:33], [[16, 15]], 8)
    iota("rown", T.rown[:], [[1, 48]], -16)
    stretches = runs(order)
    for m, first, step, n in stretches:
        iota("rowp%d" % m, T.rowp[:, 16 * m:16 * (m + n)], [[32 * step, n], [1, 16]], 32 * first)
    rowp = ["rowp%d" % r[0] for r in stretches]
    fill("ones", T.ones[:], 1.0)
    keep(["ones"], "iden", T.iden[:], T.ones[:], [[-1, 128]], A.is_equal, 0.0, 0, 1)
    for i, c in enumerate((0.5 - STEP[0] // 2, -(STEP[1] // 2), 0.5, -STEP[1])):
        fill(k("low", i), T.low[:, 64 * i:64 * i + 64], float(c))
    fill("mix", T.mix[:], 0.0)
    fill("cA", T.cA[:], 1.0)
    fill("cB1", T.cB[:, 15:16], 120.0)
    fill("mix", T.mix[:, 1::2], 1.0 / STEP[1] - 1)
    fill("cA", T.cA[:, 16:18], 0.0)
    cp(["ip"], ["p"], fc(0), T.ip[:])
    ts(["ip"], ["i0"], T.cI[:, 0:1], T.ip[:], 15, None, A.bitwise_and)
    ts(["ip"], ["i1"], T.cI[:, 1:2], T.ip[:], 4, None, A.logical_shift_right)
    fill("lU3", T.lU[:, 17:18], 32.0)
    cp(["i0", "i1"], ["sg"], T.cF[:, 1:3], T.cI[:])
    s_, g_ = fc(1), fc(2)
    sq = lambda i: T.sq[:, 128 * i:128 * i + 128]
    act(["rowm"], ["sq0"], sq(0), T.rowm[0:1, :], F.Square, scale=16.0)
    act(["rowg"], ["sq1"], sq(1), T.rowg[0:1, :], F.Square, scale=16.0)
    act(["rowg"], ["sq2"], sq(2), T.rowg[0:1, :], F.Square, scale=16.0, bias=128.0)
    idn(["sg"], ["sub"], fc(3), s_, -4096.0, 15.0 * 4096)
    idn(["sg"], ["s2"], fc(5), s_, 2.0, -15.0)

    ts(["rowg", "p"], ["expd"], T.expd[:], T.rowg[0:8, :], fc(0, 8), None, A.is_equal)
    ts(["posI"], ["posN"], T.posN[:], T.posI[:], -8.0, -32.0, A.add, A.mult)
    ts(["posI"], ["posM"], T.posM[:], T.posI[:], -8.0, -1.0 / 32, A.add, A.mult)
    lp = lambda t: (T.lp[:, 128 * t:128 * t + 128], k("lp", t))
    for t in range(2):
        ts(["expd", "posN"], [lp(t)[1]], lp(t)[0], T.expd[:], T.posN[:, t:t + 1], None, A.mult)
    one, low = T.ones[0:1, :], lambda i, n: T.low[:, 64 * i:64 * i + n]
    qq = [(lp(t)[0], T.posM[:, t:t + 1], [lp(t)[1], "posM"]) for t in range(2)]
    cells = lambda h: T["b%d" % (6 + h)][:, 0:128]
    fixed = lambda h: [(one, sq(0), ["ones", "sq0"]), (one, sq(1 + h), ["ones", k("sq", 1 + h)])]
    moved = lambda h: [(lp(0)[0], T.rowm[0:8, :], ["lp0", "rowm"]), (lp(1)[0], (T.rowg[0:8, :], T.rowh[:])[h], ["lp1", "rowg", "rowh"][:2 + h])]
    mm("b4", group(T.b4[:, 0:1], [(sq(0), T.ones[0:1, 0:1], ["sq0", "ones"]), (one, low(0, 1), ["low0"])], stop=False))
    mm("b3", group(T.b3[:, 0:1], [(T.rowm[0:1, :], low(3, 1), ["rowm", "low3"]), (one, low(1, 1), ["low1"]), (one, low(2, 1), ["low2"])], stop=False))
    mm("b5", group(T.b5[:, 64:80], [(one, T.sq[:, 0:16], ["sq0"])], stop=False))
    mm("b6", group(cells(0), fixed(0), stop=False))
    mm("b0", [(T.b0[:, t:t + 1], lp(t)[0], T.ones[0:8, 0:1], True, True, [lp(t)[1]]) for t in range(2)])
    mm("b4", group(T.b4[:, 0:1], qq, start=False))
    mm("b5", group(T.b5[:, 64:80], [(lp(1)[0], T.rowm[0:8, 0:16], ["lp1"])], start=False))
    mm("b3", group(T.b3[:, 0:1], qq, start=False))
    mm("b6", group(cells(0), moved(0), start=False))
    mm("b7", group(cells(1), fixed(1) + moved(1)))
    ts(["rowg", "sg"], ["bone"], T.bone[:], T.rowg[:], g_, None, A.is_equal)
    ts(["rowm", "sg"], ["dsc0"], T.dsc[:], T.rowm[:], s_, 18.0 * 4096, A.is_gt, A.mult)
    idn(["posI", "posN"], ["xy8"], T.xy8[:], T.posN[:], 1.0 / 32, -8.0)
    idn(["dsc0"], ["dsc"], T.dsc[:], T.dsc[:], 1.0, -17.0 * 4096)

    row = lambda h: ts(["b%d" % (6 + h), "b3"], [k("pmi", h)], H("pmi", h), cells(h), T.b3[:, 0:1], 1.0 / STEP[1], A.add, A.mult)
    mask = lambda h: ts([k("pmi", h)], [k("pm", h)], H("pm", h), H("pmi", h), 0.0, None, A.is_equal)
    ts(["b0", "b4", "sg"], ["c1"], T.dx2[:, 0:1], T.b0[:, 0:1], s_, T.b4[:, 0:1], A.mult, A.add)
    row(0)
    ts(["b5", "c1"], ["il1"], T.il1[:], T.b5[:, 64:80], T.dx2[:, 0:1], 1.0 / STEP[0], A.add, A.mult)
    mask(0)
    ts(["il1"], ["cl"], T.cl[:], T.il1[:], 511, None, A.bitwise_and)
    row(1)
    cp(["cl"], ["o1"], T.o1[:], T.cl[:])
    mask(1)
    idn(["xy8", "cB0", "cB1", "cB2"], ["lU0"], T.lU[:, 0:16], T.cB[:, 0:16], 1.0, T.xy8[:, 0:1])
    idn(["xy8", "cB2"], ["lU1"], T.lU[:, 18:33], T.cB[:, 18:33], 1.0, T.xy8[:, 0:1])
    idn(["xy8"], ["lU2"], T.lU[:, 16:17], T.xy8[:, 1:2], 1.0, 8.0)
    idn(["b0"], ["xy"], T.xy[:], T.b0[:, 0:2], 1.0 / 32, -8.0)
    mm("b4", group(T.b4[0:33, 0:128], [(T.lU[:], T.expd[:], ["lU0", "lU1", "lU2", "lU3"]), (T.cA[:], T.rowm[0:1, :], ["cA"])]))
    act(["sg", "xy"], ["dxf"], T.dx2[:, 1:2], s_, F.Square, bias=T.xy[:, 0:1])
    for h in range(2):
        tt(["tauI", "o1", k("pm", h)], [k("gm", h)], H("gm", h), T.tauI[:].indirect(T.o1[:, 8 * h:8 * h + 8]), H("pm", h), A.mult)
        mm("b%d" % (1 + h), group(T["b%d" % (1 + h)][:, 0:128], [(T.bone[:], H("gm", h), ["bone", k("gm", h)])]))
    narrow = lambda h: cp(["tauI"], [k("tauU", h)], T.tauU[:, 256 * h:256 * h + 256], T.tauI[:, 256 * h:256 * h + 256])
    narrow(0)

    act(rowp + ["xy"], ["st0"], T.st0[:], T.rowp[:], F.Square, bias=T.xy[:, 1:2])
    act(["b4"], ["lt"], T.lt[:], T.b4[0:33, 0:128], F.Copy)
    idn(["st0", "dxf"], ["stat"], T.stat[:], T.st0[:], 1.0, T.dx2[:, 1:2])
    act(["iden"], ["idf"], T.idf[:], T.iden[:], F.Copy)

    def scan(h):
        op("V", V.tensor_tensor_scan, ["dsc", "b%d" % (1 + h)], ["sc%d" % h], H("sc", h), T.dsc[:],
           T["b%d" % (1 + h)][:, 0:128], 0.0, A.add, A.max)

    def pick(h):
        ts(["sc%d" % h, "sub"], ["o2%d" % h], T.o2[:, 8 * h:8 * h + 8], T.sc[:, 128 * h + 15:128 * h + 128:16], fc(3), None, A.subtract)
    scan(0)
    ts(["rown", "sg"], ["zs"], T.zs[:], T.rown[:], s_, None, A.is_equal)
    pick(0)
    scan(1)
    ts(["rowm", "sg"], ["enm"], T.enm[:], T.rowm[:, 0:8], g_, None, A.is_equal)
    pick(1)
    ts(["rown", "s2"], ["zo"], T.zo[:], T.rown[:, 0:33], fc(5), None, A.is_equal)

    act(["tr", "o20"], ["x10"], T.x1[:, 0:128], T.trS[:].indirect(T.o2[:, 0:8]), F.Copy)
    cp(["tr", "o21"], ["x11"], T.x1[:, 128:256], T.trS[:].indirect(T.o2[:, 8:16]))
    mm("b3", [p for Q in range(4) for p in group(T.b3[32 * Q:32 * Q + 32, 0:32], [
        (T.zs[:, 16 - 16 * j:48 - 16 * j], T.x1[:, 64 * Q + 32 * j:64 * Q + 32 * j + 32], ["zs", "x1%d" % (Q // 2)]) for j in range(2)])])

    table = []

    def compose(q, a, b):
        src, out = T.trS[:].indirect(T.tauU[:, a:b]), T.vt[:, 16 * a:16 * b]
        keys = ["tr"] + [k("tauU", h) for h in range(a // 256, (b - 1) // 256 + 1)]
        table.append("vt%d" % a)
        if q == "S":
            act(keys, table[-1:], out, src, F.Copy)
        else:
            cp(keys, table[-1:], out, src)
    cuts = [0, S1, S1 + V1, S1 + V1 + VW, S1 + V1 + 2 * VW, 512]
    compose("S", cuts[0], cuts[1])
    narrow(1)
    cp(["b3"], ["send1"], T.send1[:], T.b3[:, 0:32])
    fill("b5", T.b5[0:8, 16:18], 0.0)
    fill("zero", T.zero[:], 0.0)
    compose("V", cuts[1], cuts[2])

    slot = slice(32 * rank, 32 * rank + 32)
    off = len(topo.engines(core, T.cores[same[0]]))
    order_after("G", ["send1"], [])
    total["loc"] = write(g, topo, core, [(r, T.hop1[:], T.send1[:], sem.r1) for r in relays], sem.loc)
    total["loc"] += spread(g, topo, core, [T.cores[q] for q in same], T.land1[:, slot], T.send1[:], sem.a1d, sem.loc)
    total.update({"a1d": len(same) * off, "a1x": len(cross) * off})
    total.update({"a2%d" % m: off // (1 if m < len(cross) else share(m)) for m in range(7)})
    wrote.update({name: (name, n) for name, n in total.items() if name[0] == "a"})
    for m, first, step, n in stretches:
        c = slice(16 * m, 16 * (m + n))
        keep(["ones"], "sel%d" % m, T.sel[:, c], T.ones[0:8, c], [[step, n], [0, 16]], A.is_equal, 0.0, first, -1)
    sel = ["sel%d" % r[0] for r in stretches]
    keep(rowp, "wt0", T.wt0[:], T.rowp[0:33, :], [[0, 128]], A.is_equal, 32.0, -17, 1)
    keep(["wt0"], "wt", T.wt[:], T.wt0[:], [[0, 128]], A.not_equal, -480.0, -15, 1)

    dist = [["b0", "b1"], ["b2", "b3"]]
    for h in range(2):
        for i, b in enumerate(dist[h]):
            mm(b, group(T[b][:, 0:64], [(T.idf[:], T.stat[:, 64 * h:64 * h + 64], ["idf", "stat"])] + [
                (one, low(j, 64), []) for j in ((0,), (1, 2))[i]], stop=False))
    L = lambda land, q: land[:, 32 * q:32 * q + 32]
    mm("b4", group(T.b4[:, 0:32], [(T.iden[:], T.send1[:], ["iden", "send1"])] + [(T.iden[:], L(T.land1, q), ["a1d"]) for q in same]
                   + [(T.iden[:], L(T.land1, q), ["a1x"]) for q in cross]))
    act(["b4"], ["asq"], T.asq[:], T.b4[:, 0:32], F.Square)
    compose("S", cuts[4], cuts[5])
    mm("b5", [(T.b5[0:8, 18 * h:18 * h + 16], T.enm[:], T.asq[:, 16 * h:16 * h + 16], True, True, ["enm", "asq"]) for h in range(2)])
    op("V", V.tensor_tensor_scan, ["b5", "zero"], ["rmx"], T.rmx[:], T.b5[0:8, 0:34], T.zero[:], 0.0, A.max, A.max)
    ts(["rmx"], ["th"], T.th[:], T.rmx[:, 0:33], T.rmx[:, 33:34], None, A.is_lt)
    turned = ["b6", "b4"]
    for h in range(2):
        mm(turned[h], group(T[turned[h]][0:33, 0:64], [(T.th[:], T.sel[:, 64 * h:64 * h + 64], ["th"] + sel)]))
    compose("V", cuts[2], cuts[3])
    for h in range(2):
        c = slice(64 * h, 64 * h + 64)
        tt([turned[h], "wt"], [k("rw", h)], T.rw[:, c], T[turned[h]][0:33, 0:64], T.wt[:, c], A.mult)
        for b in dist[h]:
            mm(b, group(T[b][:, 0:64], [(T.lt[:], T.rw[:, c], ["lt", k("rw", h)])], start=False))
    compose("V", cuts[3], cuts[4])

    def lists(h, step):
        a, c = 128 * h, slice(128 * h, 128 * h + 128)
        if step < 2:
            b, big = dist[h][step], 1.5 * 2.0 ** 23 * STEP[step]
            ts([b], ["il%d%d" % (h, step)], T.il[:, a + 1 - step:a + 128:2], T[b][:, 0:64], big, big, A.add, A.subtract)
        elif step == 2:
            op("V", V.tensor_tensor_scan, ["mix", "il%d0" % h, "il%d1" % h], [k("js", h)], T.js[:, c], T.mix[:], T.il[:, c], 0.0, A.mult, A.add)
        else:
            cp([k("js", h)], [k("o3", h)], T.o3[:, 64 * h:64 * h + 64], T.js[:, a + 1:a + 128:2])

    made = {}

    def gather(q, a, b):
        if a == b:
            return
        src, out = T.vt[:].indirect(T.o3[:, a:b]), T.x2[:, 16 * a:16 * b]
        keys, w = table + ["o3%d" % (a // 64)], ["x2%d" % a]
        for h in range(a // 8, (b + 7) // 8):
            made.setdefault(h, []).append(w[0])
        if q == "S":
            act(keys, w, out, src, F.Copy)
        else:
            cp(keys, w, out, src)

    bank = ["b7", "b5", "b6", "b0"]
    samples = lambda m, h: T.x2[:, 128 * (2 * m + h):128 * (2 * m + h + 1)]

    def images(t):
        b = bank[t % 4]
        mm(b, [(T[b][:, 32 * i + h:32 * i + 32:2], samples(m, h), T.zs[:, 16:32], True, True, ["zs"] + made[2 * m + h])
               for i, m in enumerate(TURNS[t]) for h in range(2)])

    def send(t):
        ms, b = TURNS[t], bank[t % 4]
        cp([b], ["send%d" % t], T.send2[:, 32 * ms[0]:32 * ms[-1] + 32], T[b][:, 0:32 * len(ms)])
        order_after("G", ["send%d" % t], [])
        to = lambda m: ((relays[m % R], L(T.hop2, m // R), L(T.send2, m), sem["r2%d" % (m // R)]) if m < len(cross)
                        else (T.cores[order[m]], T.land2[:, slot], L(T.send2, m), sem["a2%d" % m]))
        total["loc"] += write(g, topo, core, [to(m) for m in ms], sem.loc)

    for h, step in ((0, 0), (0, 1), (1, 0), (0, 2), (1, 1), (0, 3)):
        lists(h, step)
    for t, (ms, (a, b)) in enumerate(zip(TURNS, SPLIT)):
        lo, hi = 16 * ms[0], 16 * ms[-1] + 16
        gather("S", lo, lo + a)
        gather("V", lo + a, lo + b)
        if t > 0:
            send(t - 1)
        if t == 1:
            lists(1, 3)
        gather("V", lo + b, hi)
        if t == 0:
            lists(1, 2)
        if rank != order[ms[0]]:
            images(t)

    op("V", V.tensor_reduce, ["th"], ["cnt0"], T.cnt[:, 0:1], T.th[:], X.X, A.add)
    ts(["th", "cnt0"], ["cnt1"], T.cnt[:, 1:2], T.th[:, 15:16], -2.0, T.cnt[:, 0:1], A.mult, A.add)
    ts(["p", "cnt1"], ["cnt2"], T.cnt[:, 2:3], fc(0, 8), 32.0, T.cnt[:, 1:2], A.mult, A.add)
    dma("Y", "dw", T.w[:], T.cnt[:, 2:3], ["cnt2"], ["w"])

    parts = [(T.zo[:, 1 - h:33 - h], samples(7, h), ["zo"] + made[14 + h]) for h in range(2)]
    sender = {sum(plan(T, topo, c)[:2], []).index(rank): q for q, c in enumerate(T.cores) if q != rank}
    parts += [(L(T.land2, sender[m]), T.iden[:], ["iden", "a2%d" % m]) for m in LAST]
    mm("b4", group(T.b4[0:32, 0:128], parts))
    cp(["b4"], ["yo"], T.yo[:], T.b4[0:32, 0:128])
    dma("Y", "dy", T.y[:], T.yo[:], ["yo"], ["y"])
    wait("Y", "dw", total["dw"])
    wait("Y", "dy", total["dy"])
    for name in sorted(total):
        if max(known[q].get(name, 0) for q in eng) < total[name]:
            wait("G", name, total[name])
